import numpy as np
import ml_dtypes


def mxq(x, axis, fmt="e4m3"):
    dtype, down = {"e4m3": (ml_dtypes.float8_e4m3fn, 7), "e5m2": (ml_dtypes.float8_e5m2, 14)}[fmt]
    v = np.moveaxis(np.asarray(x, np.float32).astype(ml_dtypes.bfloat16).astype(np.float64), axis, -1)
    blocks = v.reshape(v.shape[:-1] + (-1, 32))
    amax = np.abs(blocks).max(-1, keepdims=True)
    byte = np.maximum(np.where(amax > 0, np.frexp(amax)[1] - 1 + 127, 0) - down, 1)
    scale = np.exp2(byte - 127.0)
    codes = (blocks / scale).astype(np.float32).astype(dtype).astype(np.float64)
    return np.moveaxis((codes * scale).reshape(v.shape), -1, axis)


WIDE = False


def mx_kscale(k):
    if not WIDE:
        return np.ones(k)
    levels = np.array([10, -10, 5, -5, 0])
    if k % 512:
        return np.exp2(np.random.permutation(np.resize(levels, k // 32))).repeat(32)
    a = np.empty((k // 512, 16))
    for p in range(k // 512):
        a[p, :8] = np.random.permutation(np.resize(levels, 8))
        for g in range(8):
            far = levels[np.abs(levels - a[p, g]) >= 10]
            a[p, g + 8] = far[np.random.randint(len(far))]
    return np.exp2(a.ravel()).repeat(32)


def f64(x):
    return np.asarray(x).astype(np.float64)


def striped(idx):
    return np.tile(idx.reshape(-1, 16).T, (8, 1)).astype(np.uint16)


def unstriped(offs):
    return offs[:16].T.reshape(-1).astype(np.int64)


E2M1 = np.array([0.0, 0.5, 1.0, 1.5, 2.0, 3.0, 4.0, 6.0, -0.0, -0.5, -1.0, -1.5, -2.0, -3.0, -4.0, -6.0])


def pack_weight(w, fmt):
    k, n = w.shape
    w = f64(np.asarray(w, np.float32).astype(ml_dtypes.bfloat16)).reshape(k // 32, 32, n)
    amax = np.abs(w).max(1)
    if fmt == "e4m3":
        byte = np.frexp(amax)[1] - 1 + 127 - 7
    else:
        mant, ex = np.frexp(amax / 6.0)
        byte = np.where(mant > 0.5, ex, ex - 1) + 127
    byte = np.clip(np.where(amax > 0, byte, 1), 1, 254)
    scaled = (w * np.exp2(127.0 - byte)[:, None, :]).reshape(k, n).astype(np.float32)
    by_word = np.ascontiguousarray(scaled.reshape(k // 512, 128, 4, n).transpose(0, 1, 3, 2))
    if fmt == "e4m3":
        words = by_word.astype(ml_dtypes.float8_e4m3fn).view(np.uint8)
    else:
        c = by_word.astype(ml_dtypes.float4_e2m1fn).view(np.uint8) & 0xF
        words = (c[..., 0::2] | (c[..., 1::2] << 4)).reshape(k // 512, 128, 2 * n)
    return np.ascontiguousarray(words), np.ascontiguousarray(byte.astype(np.uint8).reshape(k // 512, 16, n))


def unpack_weight(words, scales, fmt):
    g, _, n = scales.shape
    words = np.ascontiguousarray(words).reshape(g, 128, n, -1)
    if fmt == "e4m3":
        vals = words.view(ml_dtypes.float8_e4m3fn).astype(np.float64)
    else:
        nib = np.empty((g, 128, n, 4), np.uint8)
        nib[..., 0::2] = words & 0xF
        nib[..., 1::2] = words >> 4
        vals = E2M1[nib]
    vals = vals * np.repeat(np.exp2(scales.astype(np.float64) - 127.0), 8, axis=1)[..., None]
    return vals.transpose(0, 1, 3, 2).reshape(g * 512, n)


def gelu(v):
    return 0.5 * v * (1.0 + np.tanh(np.sqrt(2.0 / np.pi) * (v + 0.044715 * v**3)))


def bf(x):
    return np.asarray(x, np.float32).astype(ml_dtypes.bfloat16)


def planes(Y):
    n, m = Y.shape
    b = f64(bf(Y)).reshape(n // 32, 32, m)
    amax = np.abs(b).max(1)
    byte = np.clip(np.where(amax > 0, np.frexp(amax)[1] - 1 + 127 - 7, 1), 1, 254)
    codes = (b * np.exp2(127.0 - byte)[:, None, :]).reshape(n, m).astype(np.float32).astype(ml_dtypes.float8_e4m3fn).view(np.uint8)
    words = codes.reshape(n // 512, 128, 4, m).transpose(0, 1, 3, 2)
    return np.ascontiguousarray(words), np.ascontiguousarray(byte.astype(np.uint8).reshape(n // 512, 16, m))


K, H, N, T, S, T2 = 1024, 512, 768, 4096, 1024, 2048

def setup_inputs():
    n = np.random.standard_normal
    s = mx_kscale(K)[:, None]
    u = mx_kscale(H)[:, None]
    tab_words, tab_scales = pack_weight(n((K, T)) * s, "e4m3")
    w1 = (n((K, H)) / np.sqrt(K) / s).astype(np.float32)
    w2_words, w2_scales = pack_weight(n((K, H)) / np.sqrt(K) / s, "e2m1")
    w3_words, w3_scales = pack_weight(0.6 * n((H, N)) / np.sqrt(H) / u, "e4m3")
    return {
        "tab_words": tab_words, "tab_scales": tab_scales,
        "offs": striped(np.random.permutation(T)[:S]),
        "w1": w1,
        "w2_words": w2_words, "w2_scales": w2_scales,
        "gain": (np.exp(0.3 * n(H)) * u[:, 0]).astype(np.float32),
        "wgs": np.exp(0.3 * n((128, S))).astype(np.float32),
        "offs2": striped(np.random.permutation(T2)[:S]),
        "page0": (n((H, T2)) * u).astype(np.float32),
        "w3_words": w3_words, "w3_scales": w3_scales,
    }

def reference(tab_words, tab_scales, offs, w1, w2_words, w2_scales, gain, wgs, offs2, page0, w3_words, w3_scales):
    v = unpack_weight(tab_words, tab_scales, "e4m3")[:, unstriped(offs)]
    a = mxq(f64(w1), 0, "e4m3").T @ v
    b = unpack_weight(w2_words, w2_scales, "e2m1").T @ v
    h = f64(gain)[:, None] * (np.tanh(a) - np.tanh(b))
    page = f64(page0).copy()
    page[:, unstriped(offs2)] = np.tile(f64(wgs), (H // 128, 1)) * h
    e = unpack_weight(w3_words, w3_scales, "e4m3").T @ mxq(page, 0, "e4m3")
    y = e + e ** 3
    words, scales = planes(page)
    return y, page, words, scales

@@ -1,0 +1,246 @@
+from contextlib import ExitStack
+
+import concourse.mybir as mybir
+from concourse.masks import make_identity
+
+K, H, N, T, S, T2 = 1024, 512, 768, 4096, 1024, 2048
+FLOPS = 2 * 2 * K * H * S + 2 * H * N * T2
+
+F32 = mybir.dt.float32
+BF16 = mybir.dt.bfloat16
+I32 = mybir.dt.int32
+U32 = mybir.dt.uint32
+U16 = mybir.dt.uint16
+U8 = mybir.dt.uint8
+E4M3X4 = mybir.dt.float8_e4m3fn_x4
+E2M1X4 = mybir.dt.float4_e2m1fn_x4
+ACT = mybir.ActivationFunctionType
+ALU = mybir.AluOpType
+
+P = 128
+PACK = 4
+K_PASS = P * PACK
+PASSES = K // K_PASS
+QUADRANTS = 4
+QUADRANT = P // QUADRANTS
+SCALE_ROWS = 4
+LIST_ROWS = 16
+BANK = 512
+BLOCKS = S // P
+CHUNKS = T2 // BANK
+STORE_CHUNKS = 2
+ROW_STEP = 4
+HALF = S // 2
+QUARTER = S // 4
+
+
+def load_scale_rows(queue, plane, scales):
+    for q in range(QUADRANTS):
+        rows = scales[:, q * SCALE_ROWS : (q + 1) * SCALE_ROWS, :].rearrange("a r c -> r a c")
+        queue.dma_start(
+            out=plane[q * QUADRANT : q * QUADRANT + SCALE_ROWS, :, :].bitcast(I32), in_=rows.bitcast(I32)
+        )
+
+
+def entries(first, count):
+    return slice(first // LIST_ROWS, (first + count) // LIST_ROWS)
+
+
+def tile_list_vault_retest_kernel(
+    tc, tab_words, tab_scales, offs, w1, w2_words, w2_scales, gain, wgs, offs2, page0, w3_words, w3_scales,
+    out_0, out_1, out_2, out_3,
+):
+    nc = tc.nc
+    with ExitStack() as ctx:
+        keep = ctx.enter_context(tc.tile_pool(name="keep", bufs=1))
+        ring = ctx.enter_context(tc.tile_pool(name="ring", bufs=1))
+        psum = ctx.enter_context(tc.psum_pool(name="psum", bufs=8))
+
+        gather_list = keep.tile([P, S // LIST_ROWS], U16)
+        nc.sync.dma_start(gather_list[:], offs)
+        scatter_list = keep.tile([P, S // LIST_ROWS], U16)
+        nc.sync.dma_start(scatter_list[:], offs2)
+        gains = keep.tile([P, PACK], F32)
+        nc.sync.dma_start(gains[:], gain.rearrange("(p t) -> p t", t=PACK))
+        w2 = keep.tile([P, PASSES, 2 * H], U8, align_bytes=64)
+        nc.sync.dma_start(w2[:].bitcast(I32), w2_words.rearrange("a p c -> p a c").bitcast(I32))
+
+        w1_pieces = [(0, 0, H), (1, 0, H // 2), (1, H // 2, H // 2)]
+        w1_raw = [keep.tile([P, PACK, width], F32, name=f"w1_raw{a}_{c0}") for a, c0, width in w1_pieces]
+
+        def load_w1(piece):
+            a, c0, width = w1_pieces[piece]
+            rows = w1[a * K_PASS : (a + 1) * K_PASS, c0 : c0 + width]
+            nc.sync.dma_start(w1_raw[piece][:], rows.rearrange("(p i) c -> p i c", i=PACK))
+
+        load_w1(0)
+
+        tab_rows = keep.tile([P, T], U8)
+        v_plane = keep.tile([P, PASSES, S], U8, align_bytes=64)
+        w2_plane = keep.tile([P, PASSES, H], U8, align_bytes=64)
+        w3_plane = keep.tile([P, 1, N], U8, align_bytes=64)
+        nc.gpsimd.memset(tab_rows[:, : T // 2].bitcast(I32), 0)
+        nc.vector.memset(tab_rows[:, T // 2 :].bitcast(I32), 0)
+        nc.sync.dma_start(
+            tab_rows[0:P:ROW_STEP, :].bitcast(I32), tab_scales.rearrange("a q c -> q a c").bitcast(I32)
+        )
+        nc.vector.memset(w2_plane[:].bitcast(I32), 0)
+        load_scale_rows(nc.sync, w2_plane, w2_scales)
+        nc.vector.memset(v_plane[:].bitcast(I32), 0)
+        identity = keep.tile([P, P], F32)
+        make_identity(nc, identity[:])
+
+        tab = []
+        for a in range(PASSES):
+            words = keep.tile([P, T], U32, name=f"tab{a}")
+            nc.sync.dma_start(words[:].bitcast(I32), tab_words[a].rearrange("p t i -> p (t i)").bitcast(I32))
+            tab.append(words)
+        load_w1(1)
+        load_w1(2)
+
+        wgs_rows = wgs.rearrange("(m t) j -> m t j", t=PACK)
+        page_rows = page0.rearrange("(p t) c -> t p c", t=PACK)
+        out_rows = out_1.rearrange("(p t) c -> t p c", t=PACK)
+        wgs_groups = [(0, 1), (1, 1), (2, 2)]
+        pages = [keep.tile([P, T2], F32, name=f"page{t}") for t in range(PACK)]
+        weights = []
+        for t0, count in wgs_groups:
+            group = keep.tile([P, count, S], F32, name=f"wgs{t0}")
+            for q in (0, 2, 1, 3):
+                nc.sync.dma_start(group[q * QUADRANT : (q + 1) * QUADRANT], wgs_rows[:, t0 : t0 + count, :])
+            for t in range(t0, t0 + count):
+                nc.sync.dma_start(pages[t][:], page_rows[t])
+                weights.append(group[:, t - t0, :])
+        w3 = keep.tile([P, N], U32, align_bytes=64)
+        nc.sync.dma_start(w3[:].bitcast(I32), w3_words[0].rearrange("p c i -> p (c i)").bitcast(I32))
+        nc.vector.memset(w3_plane[:].bitcast(I32), 0)
+        load_scale_rows(nc.sync, w3_plane, w3_scales)
+
+        v_rows = keep.tile([P, S], U8)
+        nc.vector.tensor_copy(v_rows[:], tab_rows[:].indirect(gather_list[:]))
+        for q in range(QUADRANTS):
+            nc.gpsimd.dma_start(
+                v_plane[q * QUADRANT : q * QUADRANT + SCALE_ROWS, :, :].bitcast(I32),
+                v_rows[q * QUADRANT : (q + 1) * QUADRANT : ROW_STEP, :].bitcast(I32),
+            )
+
+        def gather_words(a, half, tag):
+            words = ring.tile([P, HALF], U32, name=tag, tag=tag, align_bytes=64)
+            nc.vector.tensor_copy(words[:], tab[a][:].indirect(gather_list[:, entries(half * HALF, HALF)]))
+            return words
+
+        v_words = {(a, half): gather_words(a, half, f"v{a}{half}") for a, half in ((0, 0), (0, 1), (1, 0))}
+
+        w1_codes = [keep.tile([P, H], U32, name=f"w1_codes{a}", align_bytes=64) for a in range(PASSES)]
+        w1_plane = [keep.tile([P, H], U8, name=f"w1_plane{a}", align_bytes=64) for a in range(PASSES)]
+        for (a, c0, width), raw, tag in zip(w1_pieces, w1_raw, ("w1a", "w1b", "last")):
+            woven = ring.tile([P, width, PACK], BF16, name=tag, tag=tag, align_bytes=64)
+            nc.vector.tensor_copy(
+                woven[:].rearrange("p (c n) i -> p c i n", n=4), raw[:].rearrange("p i (c n) -> p c i n", n=4)
+            )
+            nc.vector.quantize_mx(
+                out=w1_codes[a][:, c0 : c0 + width].bitcast(E4M3X4),
+                scales=w1_plane[a][:, c0 : c0 + width],
+                in_=woven[:].rearrange("p c i -> p (c i)"),
+            )
+        v_words[1, 1] = gather_words(1, 1, "last")
+
+        def view(block, weight_codes, weight_plane, sign, tag):
+            half, c0 = divmod(block * P, HALF)
+            bank = psum.tile([P, H], F32, name="bank", tag="bank")
+            for a in range(PASSES):
+                nc.tensor.matmul_mx(
+                    out=bank[:],
+                    lhsT=v_words[a, half][:, c0 : c0 + P].bitcast(E4M3X4),
+                    lhsT_scale=v_plane[:, a, block * P : (block + 1) * P],
+                    rhs=weight_codes[a],
+                    rhs_scale=weight_plane[a],
+                    start=(a == 0),
+                    stop=(a == PASSES - 1),
+                )
+            tanh = ring.tile([P, PACK, P], F32, name=tag, tag=tag, bufs=BLOCKS)
+            nc.scalar.activation(tanh[:], bank[:].rearrange("p (m t) -> p t m", t=PACK), ACT.Tanh, scale=sign)
+            return tanh
+
+        w1_ops = [w1_codes[a][:].bitcast(E4M3X4) for a in range(PASSES)], [w1_plane[a][:] for a in range(PASSES)]
+        w2_ops = [w2[:, a, :].bitcast(E2M1X4) for a in range(PASSES)], [w2_plane[:, a, :] for a in range(PASSES)]
+        plus, minus = {}, {}
+
+        def scatter(t, first, count):
+            bank = psum.tile([P, count], F32, name="bank", tag="bank")
+            for b in range(count // P):
+                block = first // P + b
+                cols = slice(b * P, (b + 1) * P)
+                for term, opens in ((minus[block], True), (plus[block], False)):
+                    nc.tensor.matmul(
+                        bank[:, cols], lhsT=term[:, t, :], rhs=identity[:], is_transpose=True,
+                        start=opens, stop=not opens,
+                    )
+            h = keep.tile([P, count], F32, name=f"h{t}_{first}")
+            nc.scalar.activation(h[:], bank[:], ACT.Copy, scale=gains[:, t : t + 1])
+            nc.vector.tensor_tensor(
+                pages[t][:].indirect(scatter_list[:, entries(first, count)]),
+                h[:], weights[t][:, first : first + count], ALU.mult,
+            )
+
+        for h0 in range(0, S, HALF):
+            for block in range(h0 // P, (h0 + HALF) // P):
+                minus[block] = view(block, *w2_ops, -1.0, "minus")
+            for first in range(h0, h0 + HALF, QUARTER):
+                for block in range(first // P, (first + QUARTER) // P):
+                    plus[block] = view(block, *w1_ops, 1.0, "plus")
+                scatter(0, first, QUARTER)
+            scatter(1, h0, HALF)
+        for t in range(2, PACK):
+            for h0 in range(0, S, HALF):
+                scatter(t, h0, HALF)
+
+        pairs = [keep.tile([P, 2, BANK, 2], BF16, name=f"pairs{c}") for c in range(CHUNKS)]
+        for t in range(PACK):
+            nc.sync.dma_start(out_rows[t], pages[t][:])
+            for c in range(CHUNKS):
+                nc.scalar.copy(pairs[c][:, t // 2, :, t % 2], pages[t][:, c * BANK : (c + 1) * BANK])
+
+        page_codes = keep.tile([P, T2], U32, align_bytes=64)
+        page_plane = keep.tile([P, T2], U8, align_bytes=64)
+        codes_out = out_2[0].rearrange("p m t -> p (m t)").bitcast(I32)
+        for c in range(CHUNKS):
+            cols = slice(c * BANK, (c + 1) * BANK)
+            woven = ring.tile([P, BANK, 2], F32, name="woven", tag="woven", bufs=2, align_bytes=64)
+            words = pairs[c][:].rearrange("p u c e -> p u (c e)").bitcast(F32)
+            nc.vector.tensor_copy(woven[:], words.rearrange("p u c -> p c u"))
+            nc.vector.quantize_mx(
+                out=page_codes[:, cols].bitcast(E4M3X4),
+                scales=page_plane[:, cols],
+                in_=woven[:].rearrange("p c u -> p (c u)").bitcast(BF16),
+            )
+        span = STORE_CHUNKS * BANK
+        for c0 in range(0, T2, span):
+            nc.sync.dma_start(codes_out[:, c0 : c0 + span], page_codes[:, c0 : c0 + span].bitcast(I32))
+        for q in range(QUADRANTS):
+            nc.sync.dma_start(
+                out_3[0, q * SCALE_ROWS : (q + 1) * SCALE_ROWS, :].bitcast(I32),
+                page_plane[q * QUADRANT : q * QUADRANT + SCALE_ROWS, :].bitcast(I32),
+            )
+
+        for c0 in range(0, T2, span):
+            for n0 in range(0, N, P):
+                y = ring.tile([P, span], F32, name="y", tag="y", bufs=5)
+                for c1 in range(0, span, BANK):
+                    cols = slice(c0 + c1, c0 + c1 + BANK)
+                    e = psum.tile([P, BANK], F32, name="bank", tag="bank")
+                    nc.tensor.matmul_mx(
+                        out=e[:],
+                        lhsT=w3[:, n0 : n0 + P].bitcast(E4M3X4),
+                        lhsT_scale=w3_plane[:, 0, n0 : n0 + P],
+                        rhs=page_codes[:, cols].bitcast(E4M3X4),
+                        rhs_scale=page_plane[:, cols],
+                        start=True,
+                        stop=True,
+                    )
+                    square = ring.tile([P, BANK], F32, name="minus", tag="minus", bufs=BLOCKS)
+                    nc.scalar.activation(square[:], e[:], ACT.Square)
+                    nc.vector.scalar_tensor_tensor(
+                        y[:, c1 : c1 + BANK], square[:], 1.0, e[:], ALU.add, ALU.mult
+                    )
+                nc.sync.dma_start(out_0[n0 : n0 + P, c0 : c0 + span], y[:])

@@ -30,6 +30,8 @@ BLOCKS = S // P
 CHUNKS = T2 // BANK
 STORE_CHUNKS = 2
 ROW_STEP = 4
+BANKS = 8
+VIEW_BANKS = 3
 HALF = S // 2
 QUARTER = S // 4
 
@@ -54,7 +56,7 @@ def tile_list_vault_retest_kernel(
     with ExitStack() as ctx:
         keep = ctx.enter_context(tc.tile_pool(name="keep", bufs=1))
         ring = ctx.enter_context(tc.tile_pool(name="ring", bufs=1))
-        psum = ctx.enter_context(tc.psum_pool(name="psum", bufs=8))
+        psum = ctx.enter_context(tc.psum_pool(name="psum", bufs=1))
 
         gather_list = keep.tile([P, S // LIST_ROWS], U16)
         nc.sync.dma_start(gather_list[:], offs)
@@ -65,89 +67,106 @@ def tile_list_vault_retest_kernel(
         w2 = keep.tile([P, PASSES, 2 * H], U8, align_bytes=64)
         nc.sync.dma_start(w2[:].bitcast(I32), w2_words.rearrange("a p c -> p a c").bitcast(I32))
 
-        w1_pieces = [(0, 0, H), (1, 0, H // 2), (1, H // 2, H // 2)]
-        w1_raw = [keep.tile([P, PACK, width], F32, name=f"w1_raw{a}_{c0}") for a, c0, width in w1_pieces]
-
-        def load_w1(piece):
-            a, c0, width = w1_pieces[piece]
-            rows = w1[a * K_PASS : (a + 1) * K_PASS, c0 : c0 + width]
-            nc.sync.dma_start(w1_raw[piece][:], rows.rearrange("(p i) c -> p i c", i=PACK))
-
-        load_w1(0)
-
-        tab_rows = keep.tile([P, T], U8)
-        v_plane = keep.tile([P, PASSES, S], U8, align_bytes=64)
-        w2_plane = keep.tile([P, PASSES, H], U8, align_bytes=64)
-        w3_plane = keep.tile([P, 1, N], U8, align_bytes=64)
+        tab_rows = ring.tile([P, T], U8, tag="tab1")
         nc.gpsimd.memset(tab_rows[:, : T // 2].bitcast(I32), 0)
         nc.vector.memset(tab_rows[:, T // 2 :].bitcast(I32), 0)
         nc.sync.dma_start(
             tab_rows[0:P:ROW_STEP, :].bitcast(I32), tab_scales.rearrange("a q c -> q a c").bitcast(I32)
         )
+
+        w1_rows = w1.rearrange("(a p i) c -> a p i c", a=PASSES, i=PACK)
+        w1_first = ring.tile([P, PACK, H], F32, tag="w1_raw")
+        nc.sync.dma_start(w1_first[:], w1_rows[0])
+
+        v_plane = keep.tile([P, PASSES, S], U8, align_bytes=64)
+        w2_plane = keep.tile([P, PASSES, H], U8, align_bytes=64)
+        w3_plane = keep.tile([P, 1, N], U8, align_bytes=64)
         nc.vector.memset(w2_plane[:].bitcast(I32), 0)
         load_scale_rows(nc.sync, w2_plane, w2_scales)
         nc.vector.memset(v_plane[:].bitcast(I32), 0)
         identity = keep.tile([P, P], F32)
         make_identity(nc, identity[:])
 
-        tab = []
-        for a in range(PASSES):
-            words = keep.tile([P, T], U32, name=f"tab{a}")
-            nc.sync.dma_start(words[:].bitcast(I32), tab_words[a].rearrange("p t i -> p (t i)").bitcast(I32))
-            tab.append(words)
-        load_w1(1)
-        load_w1(2)
+        tab = {}
+
+        def load_tab(a):
+            tab[a] = ring.tile([P, T], U32, name=f"tab{a}", tag=f"tab{a}")
+            nc.sync.dma_start(tab[a][:].bitcast(I32), tab_words[a].rearrange("p t i -> p (t i)").bitcast(I32))
+
+        load_tab(0)
 
         wgs_rows = wgs.rearrange("(m t) j -> m t j", t=PACK)
         page_rows = page0.rearrange("(p t) c -> t p c", t=PACK)
         out_rows = out_1.rearrange("(p t) c -> t p c", t=PACK)
-        wgs_groups = [(0, 1), (1, 1), (2, 2)]
-        pages = [keep.tile([P, T2], F32, name=f"page{t}") for t in range(PACK)]
-        weights = []
-        for t0, count in wgs_groups:
-            group = keep.tile([P, count, S], F32, name=f"wgs{t0}")
-            for q in (0, 2, 1, 3):
-                nc.sync.dma_start(group[q * QUADRANT : (q + 1) * QUADRANT], wgs_rows[:, t0 : t0 + count, :])
-            for t in range(t0, t0 + count):
-                nc.sync.dma_start(pages[t][:], page_rows[t])
-                weights.append(group[:, t - t0, :])
-        w3 = keep.tile([P, N], U32, align_bytes=64)
-        nc.sync.dma_start(w3[:].bitcast(I32), w3_words[0].rearrange("p c i -> p (c i)").bitcast(I32))
         nc.vector.memset(w3_plane[:].bitcast(I32), 0)
-        load_scale_rows(nc.sync, w3_plane, w3_scales)
+        load_scale_rows(nc.gpsimd, w3_plane, w3_scales)
 
-        v_rows = keep.tile([P, S], U8)
+        v_rows = ring.tile([P, S], U8, tag="v_rows", align_bytes=64)
         nc.vector.tensor_copy(v_rows[:], tab_rows[:].indirect(gather_list[:]))
         for q in range(QUADRANTS):
-            nc.gpsimd.dma_start(
+            nc.sync.dma_start(
                 v_plane[q * QUADRANT : q * QUADRANT + SCALE_ROWS, :, :].bitcast(I32),
                 v_rows[q * QUADRANT : (q + 1) * QUADRANT : ROW_STEP, :].bitcast(I32),
             )
+
+        load_tab(1)
 
         def gather_words(a, half, tag):
             words = ring.tile([P, HALF], U32, name=tag, tag=tag, align_bytes=64)
             nc.vector.tensor_copy(words[:], tab[a][:].indirect(gather_list[:, entries(half * HALF, HALF)]))
             return words
 
-        v_words = {(a, half): gather_words(a, half, f"v{a}{half}") for a, half in ((0, 0), (0, 1), (1, 0))}
-
         w1_codes = [keep.tile([P, H], U32, name=f"w1_codes{a}", align_bytes=64) for a in range(PASSES)]
         w1_plane = [keep.tile([P, H], U8, name=f"w1_plane{a}", align_bytes=64) for a in range(PASSES)]
-        for (a, c0, width), raw, tag in zip(w1_pieces, w1_raw, ("w1a", "w1b", "last")):
+
+        def quantise_w1(a, c0, raw, tag):
+            width = raw.shape[2]
             woven = ring.tile([P, width, PACK], BF16, name=tag, tag=tag, align_bytes=64)
             nc.vector.tensor_copy(
-                woven[:].rearrange("p (c n) i -> p c i n", n=4), raw[:].rearrange("p i (c n) -> p c i n", n=4)
+                woven[:].rearrange("p (c n) i -> p c i n", n=4), raw.rearrange("p i (c n) -> p c i n", n=4)
             )
             nc.vector.quantize_mx(
                 out=w1_codes[a][:, c0 : c0 + width].bitcast(E4M3X4),
                 scales=w1_plane[a][:, c0 : c0 + width],
                 in_=woven[:].rearrange("p c i -> p (c i)"),
             )
+
+        quantise_w1(0, 0, w1_first[:], "w1a")
+        w1_second = ring.tile([P, 2, PACK, H // 2], F32, tag="w1_raw")
+        for u in range(2):
+            nc.sync.dma_start(w1_second[:, u], w1_rows[1][:, :, u * H // 2 : (u + 1) * H // 2])
+        v_words = {(a, half): gather_words(a, half, f"v{a}{half}") for a, half in ((0, 0), (0, 1), (1, 0))}
+        quantise_w1(1, 0, w1_second[:, 0], "w1b")
+        quantise_w1(1, H // 2, w1_second[:, 1], "last")
         v_words[1, 1] = gather_words(1, 1, "last")
+
+        pages, weights = {}, {}
+
+        def load_page(t, tag):
+            pages[t] = ring.tile([P, T2], F32, name=f"page{t}", tag=tag, align_bytes=64)
+            nc.sync.dma_start(pages[t][:], page_rows[t])
+
+        def load_wgs(tile, slices, first):
+            for q in (0, 2, 1, 3):
+                rows = wgs_rows[:, slices.start : slices.stop, first : first + tile.shape[2]]
+                nc.sync.dma_start(tile[q * QUADRANT : (q + 1) * QUADRANT], rows)
+            for t in slices:
+                for h0 in range(0, tile.shape[2], HALF):
+                    weights[t, first + h0] = tile[:, t - slices.start, h0 : h0 + HALF]
+
+        load_page(0, "v_rows")
+        early = ring.tile([P, 2, HALF], F32, tag="tab0")
+        load_wgs(early[:, 0:1, :], range(0, 1), 0)
+        load_wgs(early[:, 1:2, :], range(1, 2), 0)
+        load_page(1, "w1b")
+        middle = ring.tile([P, 2, HALF], F32, tag="w1_raw")
+        load_wgs(middle[:], range(0, 2), HALF)
+        late = ring.tile([P, 2, S], F32, tag="tab1")
+        load_wgs(late[:], range(2, PACK), 0)
 
         def view(block, weight_codes, weight_plane, sign, tag):
             half, c0 = divmod(block * P, HALF)
-            bank = psum.tile([P, H], F32, name="bank", tag="bank")
+            bank = psum.tile([P, H], F32, name="bank", tag="view", bufs=VIEW_BANKS)
             for a in range(PASSES):
                 nc.tensor.matmul_mx(
                     out=bank[:],
@@ -167,7 +186,7 @@ def tile_list_vault_retest_kernel(
         plus, minus = {}, {}
 
         def scatter(t, first, count):
-            bank = psum.tile([P, count], F32, name="bank", tag="bank")
+            bank = psum.tile([P, count], F32, name="bank", tag="diff", bufs=BANKS - VIEW_BANKS)
             for b in range(count // P):
                 block = first // P + b
                 cols = slice(b * P, (b + 1) * P)
@@ -176,21 +195,26 @@ def tile_list_vault_retest_kernel(
                         bank[:, cols], lhsT=term[:, t, :], rhs=identity[:], is_transpose=True,
                         start=opens, stop=not opens,
                     )
-            h = keep.tile([P, count], F32, name=f"h{t}_{first}")
+            h = ring.tile([P, count], F32, name="h", tag=f"h{t}_{first}", align_bytes=64)
             nc.scalar.activation(h[:], bank[:], ACT.Copy, scale=gains[:, t : t + 1])
             nc.vector.tensor_tensor(
                 pages[t][:].indirect(scatter_list[:, entries(first, count)]),
-                h[:], weights[t][:, first : first + count], ALU.mult,
+                h[:], weights[t, first // HALF * HALF][:, first % HALF : first % HALF + count], ALU.mult,
             )
 
         for h0 in range(0, S, HALF):
-            for block in range(h0 // P, (h0 + HALF) // P):
-                minus[block] = view(block, *w2_ops, -1.0, "minus")
             for first in range(h0, h0 + HALF, QUARTER):
-                for block in range(first // P, (first + QUARTER) // P):
+                blocks = range(first // P, (first + QUARTER) // P)
+                for block in blocks:
+                    minus[block] = view(block, *w2_ops, -1.0, "minus")
+                for block in blocks:
                     plus[block] = view(block, *w1_ops, 1.0, "plus")
                 scatter(0, first, QUARTER)
             scatter(1, h0, HALF)
+        load_page(2, "h0_0")
+        load_page(3, f"h0_{QUARTER}")
+        w3 = ring.tile([P, N], U32, tag="h1_0", align_bytes=64)
+        nc.sync.dma_start(w3[:].bitcast(I32), w3_words[0].rearrange("p c i -> p (c i)").bitcast(I32))
         for t in range(2, PACK):
             for h0 in range(0, S, HALF):
                 scatter(t, h0, HALF)
@@ -225,10 +249,11 @@ def tile_list_vault_retest_kernel(
 
         for c0 in range(0, T2, span):
             for n0 in range(0, N, P):
-                y = ring.tile([P, span], F32, name="y", tag="y", bufs=5)
+                y = ring.tile([P, span], F32, name="y", tag="y", bufs=8)
                 for c1 in range(0, span, BANK):
                     cols = slice(c0 + c1, c0 + c1 + BANK)
-                    e = psum.tile([P, BANK], F32, name="bank", tag="bank")
+                    tag, bufs = (("view", VIEW_BANKS), ("diff", BANKS - VIEW_BANKS))[c1 // BANK]
+                    e = psum.tile([P, BANK], F32, name="bank", tag=tag, bufs=bufs)
                     nc.tensor.matmul_mx(
                         out=e[:],
                         lhsT=w3[:, n0 : n0 + P].bitcast(E4M3X4),
@@ -243,4 +268,7 @@ def tile_list_vault_retest_kernel(
                     nc.vector.scalar_tensor_tensor(
                         y[:, c1 : c1 + BANK], square[:], 1.0, e[:], ALU.add, ALU.mult
                     )
-                nc.sync.dma_start(out_0[n0 : n0 + P, c0 : c0 + span], y[:])
+                    if (c0, n0) == (T2 - span, N - P):
+                        nc.sync.dma_start(out_0[n0 : n0 + P, cols], y[:, c1 : c1 + BANK])
+                if (c0, n0) != (T2 - span, N - P):
+                    nc.sync.dma_start(out_0[n0 : n0 + P, c0 : c0 + span], y[:])

@@ -31,7 +31,7 @@ CHUNKS = T2 // BANK
 STORE_CHUNKS = 2
 ROW_STEP = 4
 BANKS = 8
-VIEW_BANKS = 3
+STAGE_BANKS = 5
 HALF = S // 2
 QUARTER = S // 4
 
@@ -166,7 +166,7 @@ def tile_list_vault_retest_kernel(
 
         def view(block, weight_codes, weight_plane, sign, tag):
             half, c0 = divmod(block * P, HALF)
-            bank = psum.tile([P, H], F32, name="bank", tag="view", bufs=VIEW_BANKS)
+            bank = psum.tile([P, H], F32, name="bank", tag="stage", bufs=STAGE_BANKS)
             for a in range(PASSES):
                 nc.tensor.matmul_mx(
                     out=bank[:],
@@ -178,7 +178,9 @@ def tile_list_vault_retest_kernel(
                     stop=(a == PASSES - 1),
                 )
             tanh = ring.tile([P, PACK, P], F32, name=tag, tag=tag, bufs=BLOCKS)
-            nc.scalar.activation(tanh[:], bank[:].rearrange("p (m t) -> p t m", t=PACK), ACT.Tanh, scale=sign)
+            nc.scalar.activation(
+                tanh[:].rearrange("p t m -> p m t"), bank[:].rearrange("p (m t) -> p m t", t=PACK), ACT.Tanh, scale=sign
+            )
             return tanh
 
         w1_ops = [w1_codes[a][:].bitcast(E4M3X4) for a in range(PASSES)], [w1_plane[a][:] for a in range(PASSES)]
@@ -186,7 +188,7 @@ def tile_list_vault_retest_kernel(
         plus, minus = {}, {}
 
         def scatter(t, first, count):
-            bank = psum.tile([P, count], F32, name="bank", tag="diff", bufs=BANKS - VIEW_BANKS)
+            bank = psum.tile([P, count], F32, name="bank", tag="stage", bufs=STAGE_BANKS)
             for b in range(count // P):
                 block = first // P + b
                 cols = slice(b * P, (b + 1) * P)
@@ -196,18 +198,20 @@ def tile_list_vault_retest_kernel(
                         start=opens, stop=not opens,
                     )
             h = ring.tile([P, count], F32, name="h", tag=f"h{t}_{first}", align_bytes=64)
-            nc.scalar.activation(h[:], bank[:], ACT.Copy, scale=gains[:, t : t + 1])
+            if (t, first) == (0, 0):
+                nc.vector.tensor_scalar(h[:], bank[:], gains[:, t : t + 1], None, ALU.mult)
+            else:
+                nc.scalar.activation(h[:], bank[:], ACT.Copy, scale=gains[:, t : t + 1])
             nc.vector.tensor_tensor(
                 pages[t][:].indirect(scatter_list[:, entries(first, count)]),
                 h[:], weights[t, first // HALF * HALF][:, first % HALF : first % HALF + count], ALU.mult,
             )
 
         for h0 in range(0, S, HALF):
+            for block in range(h0 // P, (h0 + HALF) // P):
+                minus[block] = view(block, *w2_ops, -1.0, "minus")
             for first in range(h0, h0 + HALF, QUARTER):
-                blocks = range(first // P, (first + QUARTER) // P)
-                for block in blocks:
-                    minus[block] = view(block, *w2_ops, -1.0, "minus")
-                for block in blocks:
+                for block in range(first // P, (first + QUARTER) // P):
                     plus[block] = view(block, *w1_ops, 1.0, "plus")
                 scatter(0, first, QUARTER)
             scatter(1, h0, HALF)
@@ -223,36 +227,53 @@ def tile_list_vault_retest_kernel(
         for t in range(PACK):
             nc.sync.dma_start(out_rows[t], pages[t][:])
             for c in range(CHUNKS):
-                nc.scalar.copy(pairs[c][:, t // 2, :, t % 2], pages[t][:, c * BANK : (c + 1) * BANK])
+                rows = pages[t][:, c * BANK : (c + 1) * BANK]
+                if (c, t) == (0, PACK - 1):
+                    nc.vector.tensor_copy(pairs[c][:, t // 2, :, t % 2], rows)
+                elif (c, t) == (0, PACK - 2):
+                    nc.scalar.copy(pairs[c][:, t // 2, :, :], rows.unsqueeze(2).to_broadcast([P, BANK, 2]))
+                else:
+                    nc.scalar.copy(pairs[c][:, t // 2, :, t % 2], rows)
 
         page_codes = keep.tile([P, T2], U32, align_bytes=64)
         page_plane = keep.tile([P, T2], U8, align_bytes=64)
         codes_out = out_2[0].rearrange("p m t -> p (m t)").bitcast(I32)
-        for c in range(CHUNKS):
-            cols = slice(c * BANK, (c + 1) * BANK)
-            woven = ring.tile([P, BANK, 2], F32, name="woven", tag="woven", bufs=2, align_bytes=64)
-            words = pairs[c][:].rearrange("p u c e -> p u (c e)").bitcast(F32)
-            nc.vector.tensor_copy(woven[:], words.rearrange("p u c -> p c u"))
-            nc.vector.quantize_mx(
-                out=page_codes[:, cols].bitcast(E4M3X4),
-                scales=page_plane[:, cols],
-                in_=woven[:].rearrange("p c u -> p (c u)").bitcast(BF16),
-            )
         span = STORE_CHUNKS * BANK
-        for c0 in range(0, T2, span):
+
+        def quantise_page(c0):
+            for c in range(c0 // BANK, (c0 + span) // BANK):
+                cols = slice(c * BANK, (c + 1) * BANK)
+                woven = ring.tile([P, BANK, 2], F32, name="woven", tag="woven", bufs=2, align_bytes=64)
+                words = pairs[c][:].rearrange("p u c e -> p u (c e)").bitcast(F32).rearrange("p u c -> p c u")
+                if c == CHUNKS - 1:
+                    nc.scalar.copy(woven[:], words)
+                else:
+                    nc.vector.tensor_copy(woven[:], words)
+                nc.vector.quantize_mx(
+                    out=page_codes[:, cols].bitcast(E4M3X4),
+                    scales=page_plane[:, cols],
+                    in_=woven[:].rearrange("p c u -> p (c u)").bitcast(BF16),
+                )
+
+        def store_codes(c0):
             nc.sync.dma_start(codes_out[:, c0 : c0 + span], page_codes[:, c0 : c0 + span].bitcast(I32))
+
+        banks = [("spare", BANKS - STAGE_BANKS)] * (BANKS - STAGE_BANKS) + [("stage", STAGE_BANKS)] * STAGE_BANKS
+        for c0 in range(0, T2, span):
+            quantise_page(c0)
+            store_codes(c0)
         for q in range(QUADRANTS):
             nc.sync.dma_start(
                 out_3[0, q * SCALE_ROWS : (q + 1) * SCALE_ROWS, :].bitcast(I32),
                 page_plane[q * QUADRANT : q * QUADRANT + SCALE_ROWS, :].bitcast(I32),
             )
-
         for c0 in range(0, T2, span):
             for n0 in range(0, N, P):
                 y = ring.tile([P, span], F32, name="y", tag="y", bufs=8)
                 for c1 in range(0, span, BANK):
                     cols = slice(c0 + c1, c0 + c1 + BANK)
-                    tag, bufs = (("view", VIEW_BANKS), ("diff", BANKS - VIEW_BANKS))[c1 // BANK]
+                    turn = (c0 // span * (N // P) + n0 // P) * STORE_CHUNKS + c1 // BANK
+                    tag, bufs = banks[turn % BANKS]
                     e = psum.tile([P, BANK], F32, name="bank", tag=tag, bufs=bufs)
                     nc.tensor.matmul_mx(
                         out=e[:],

@@ -80,7 +80,6 @@ def tile_list_vault_retest_kernel(
 
         v_plane = keep.tile([P, PASSES, S], U8, align_bytes=64)
         w2_plane = keep.tile([P, PASSES, H], U8, align_bytes=64)
-        w3_plane = keep.tile([P, 1, N], U8, align_bytes=64)
         nc.vector.memset(w2_plane[:].bitcast(I32), 0)
         load_scale_rows(nc.sync, w2_plane, w2_scales)
         nc.vector.memset(v_plane[:].bitcast(I32), 0)
@@ -98,8 +97,6 @@ def tile_list_vault_retest_kernel(
         wgs_rows = wgs.rearrange("(m t) j -> m t j", t=PACK)
         page_rows = page0.rearrange("(p t) c -> t p c", t=PACK)
         out_rows = out_1.rearrange("(p t) c -> t p c", t=PACK)
-        nc.vector.memset(w3_plane[:].bitcast(I32), 0)
-        load_scale_rows(nc.gpsimd, w3_plane, w3_scales)
 
         v_rows = ring.tile([P, S], U8, tag="v_rows", align_bytes=64)
         nc.vector.tensor_copy(v_rows[:], tab_rows[:].indirect(gather_list[:]))
@@ -151,8 +148,7 @@ def tile_list_vault_retest_kernel(
                 rows = wgs_rows[:, slices.start : slices.stop, first : first + tile.shape[2]]
                 nc.sync.dma_start(tile[q * QUADRANT : (q + 1) * QUADRANT], rows)
             for t in slices:
-                for h0 in range(0, tile.shape[2], HALF):
-                    weights[t, first + h0] = tile[:, t - slices.start, h0 : h0 + HALF]
+                weights[t, first] = tile[:, t - slices.start, :]
 
         load_page(0, "v_rows")
         early = ring.tile([P, 2, HALF], F32, tag="tab0")
@@ -161,8 +157,8 @@ def tile_list_vault_retest_kernel(
         load_page(1, "w1b")
         middle = ring.tile([P, 2, HALF], F32, tag="w1_raw")
         load_wgs(middle[:], range(0, 2), HALF)
-        late = ring.tile([P, 2, S], F32, tag="tab1")
-        load_wgs(late[:], range(2, PACK), 0)
+        late = ring.tile([P, 1, S], F32, tag="tab1")
+        load_wgs(late[:], range(2, 3), 0)
 
         def view(block, weight_codes, weight_plane, sign, tag):
             half, c0 = divmod(block * P, HALF)
@@ -178,9 +174,7 @@ def tile_list_vault_retest_kernel(
                     stop=(a == PASSES - 1),
                 )
             tanh = ring.tile([P, PACK, P], F32, name=tag, tag=tag, bufs=BLOCKS)
-            nc.scalar.activation(
-                tanh[:].rearrange("p t m -> p m t"), bank[:].rearrange("p (m t) -> p m t", t=PACK), ACT.Tanh, scale=sign
-            )
+            nc.scalar.activation(tanh[:], bank[:].rearrange("p (m t) -> p t m", t=PACK), ACT.Tanh, scale=sign)
             return tanh
 
         w1_ops = [w1_codes[a][:].bitcast(E4M3X4) for a in range(PASSES)], [w1_plane[a][:] for a in range(PASSES)]
@@ -188,23 +182,25 @@ def tile_list_vault_retest_kernel(
         plus, minus = {}, {}
 
         def scatter(t, first, count):
-            bank = psum.tile([P, count], F32, name="bank", tag="stage", bufs=STAGE_BANKS)
-            for b in range(count // P):
-                block = first // P + b
-                cols = slice(b * P, (b + 1) * P)
-                for term, opens in ((minus[block], True), (plus[block], False)):
-                    nc.tensor.matmul(
-                        bank[:, cols], lhsT=term[:, t, :], rhs=identity[:], is_transpose=True,
-                        start=opens, stop=not opens,
-                    )
             h = ring.tile([P, count], F32, name="h", tag=f"h{t}_{first}", align_bytes=64)
-            if (t, first) == (0, 0):
-                nc.vector.tensor_scalar(h[:], bank[:], gains[:, t : t + 1], None, ALU.mult)
-            else:
-                nc.scalar.activation(h[:], bank[:], ACT.Copy, scale=gains[:, t : t + 1])
+            for c0 in range(0, count, BANK):
+                width = min(count, BANK)
+                bank = psum.tile([P, width], F32, name="bank", tag="stage", bufs=STAGE_BANKS)
+                for b0 in range(0, width, P):
+                    block = (first + c0 + b0) // P
+                    for term, opens in ((minus[block], True), (plus[block], False)):
+                        nc.tensor.matmul(
+                            bank[:, b0 : b0 + P], lhsT=term[:, t, :], rhs=identity[:], is_transpose=True,
+                            start=opens, stop=not opens,
+                        )
+                if (t, first) == (0, 0):
+                    nc.vector.tensor_scalar(h[:], bank[:], gains[:, t : t + 1], None, ALU.mult)
+                else:
+                    nc.scalar.activation(h[:, c0 : c0 + width], bank[:], ACT.Copy, scale=gains[:, t : t + 1])
+            w0 = max(c0 for s, c0 in weights if s == t and c0 <= first)
             nc.vector.tensor_tensor(
                 pages[t][:].indirect(scatter_list[:, entries(first, count)]),
-                h[:], weights[t, first // HALF * HALF][:, first % HALF : first % HALF + count], ALU.mult,
+                h[:], weights[t, w0][:, first - w0 : first - w0 + count], ALU.mult,
             )
 
         for h0 in range(0, S, HALF):
@@ -216,12 +212,16 @@ def tile_list_vault_retest_kernel(
                 scatter(0, first, QUARTER)
             scatter(1, h0, HALF)
         load_page(2, "h0_0")
-        load_page(3, f"h0_{QUARTER}")
-        w3 = ring.tile([P, N], U32, tag="h1_0", align_bytes=64)
+        latest = ring.tile([P, 1, S], F32, tag=f"h0_{QUARTER}", align_bytes=64)
+        load_wgs(latest[:], range(3, PACK), 0)
+        load_page(3, "h1_0")
+        w3 = ring.tile([P, N], U32, tag=f"h0_{HALF}", align_bytes=64)
         nc.sync.dma_start(w3[:].bitcast(I32), w3_words[0].rearrange("p c i -> p (c i)").bitcast(I32))
+        w3_plane = ring.tile([P, 1, N], U8, tag=f"h0_{HALF + QUARTER}", align_bytes=64)
+        nc.gpsimd.memset(w3_plane[:].bitcast(I32), 0)
+        load_scale_rows(nc.sync, w3_plane, w3_scales)
         for t in range(2, PACK):
-            for h0 in range(0, S, HALF):
-                scatter(t, h0, HALF)
+            scatter(t, 0, S)
 
         pairs = [keep.tile([P, 2, BANK, 2], BF16, name=f"pairs{c}") for c in range(CHUNKS)]
         for t in range(PACK):

@@ -29,11 +29,13 @@ BANK = 512
 BLOCKS = S // P
 CHUNKS = T2 // BANK
 STORE_CHUNKS = 2
-ROW_STEP = 4
+QUADRANT_ROWS = PASSES * SCALE_ROWS
 BANKS = 8
-STAGE_BANKS = 5
 HALF = S // 2
-QUARTER = S // 4
+FIRST = 256
+VIEW_BANKS = (2, 3, 4, 6, 1)
+DIFFERENCE_BANKS = (0, 5, 7)
+KIB = 1024
 
 
 def load_scale_rows(queue, plane, scales):
@@ -56,174 +58,196 @@ def tile_list_vault_retest_kernel(
     with ExitStack() as ctx:
         keep = ctx.enter_context(tc.tile_pool(name="keep", bufs=1))
         ring = ctx.enter_context(tc.tile_pool(name="ring", bufs=1))
+        laid = ctx.enter_context(tc.tile_pool(name="laid", bufs=1))
         psum = ctx.enter_context(tc.psum_pool(name="psum", bufs=1))
 
+        def place(name, shape, dtype, kib):
+            return laid.tile(shape, dtype, name=name, offset=int(kib * KIB), align_bytes=64)
+
+        def new_bank(width, number):
+            return psum.tile([P, width], F32, name="bank", tag=f"bank{number}")
+
+        w2_plane = keep.tile([P, PASSES, H], U8, align_bytes=64)
+        nc.vector.memset(w2_plane[:].bitcast(I32), 0)
         gather_list = keep.tile([P, S // LIST_ROWS], U16)
         nc.sync.dma_start(gather_list[:], offs)
+        tab_rows = place("tab_rows", [P, T], U8, 14)
+        nc.sync.dma_start(
+            tab_rows[:QUADRANT, :].bitcast(I32), tab_scales.rearrange("a q c -> q a c").bitcast(I32)
+        )
+        nc.gpsimd.memset(tab_rows[QUADRANT : 2 * QUADRANT, :].bitcast(I32), 0)
+        nc.vector.memset(tab_rows[2 * QUADRANT :, :].bitcast(I32), 0)
+        tab = [place("tab0", [P, T], U32, 48), place("tab1", [P, T], U32, 16)]
+        tab_hbm = [tab_words[a].rearrange("p t i -> p (t i)").bitcast(I32) for a in range(PASSES)]
+        w2 = keep.tile([P, PASSES, 2 * H], U8, align_bytes=64)
+        nc.sync.dma_start(w2[:].bitcast(I32), w2_words.rearrange("a p c -> p a c").bitcast(I32))
+
+        v_plane = keep.tile([P, PASSES, S], U8, align_bytes=64)
+        load_scale_rows(nc.sync, w2_plane, w2_scales)
+        nc.sync.dma_start(tab[0][:].bitcast(I32), tab_hbm[0])
+        nc.vector.memset(v_plane[:].bitcast(I32), 0)
+        identity = keep.tile([P, P], F32)
+        make_identity(nc, identity[:])
+        w1_rows = w1.rearrange("(a p i) c -> a p i c", a=PASSES, i=PACK)
+        w1_raw = [place(f"w1_raw{a}", [P, PACK, H], F32, 8 * a) for a in range(PASSES)]
+        nc.sync.dma_start(w1_raw[0][:], w1_rows[0])
         scatter_list = keep.tile([P, S // LIST_ROWS], U16)
         nc.sync.dma_start(scatter_list[:], offs2)
         gains = keep.tile([P, PACK], F32)
         nc.sync.dma_start(gains[:], gain.rearrange("(p t) -> p t", t=PACK))
-        w2 = keep.tile([P, PASSES, 2 * H], U8, align_bytes=64)
-        nc.sync.dma_start(w2[:].bitcast(I32), w2_words.rearrange("a p c -> p a c").bitcast(I32))
 
-        tab_rows = ring.tile([P, T], U8, tag="tab1")
-        nc.gpsimd.memset(tab_rows[:, : T // 2].bitcast(I32), 0)
-        nc.vector.memset(tab_rows[:, T // 2 :].bitcast(I32), 0)
-        nc.sync.dma_start(
-            tab_rows[0:P:ROW_STEP, :].bitcast(I32), tab_scales.rearrange("a q c -> q a c").bitcast(I32)
+        v_rows = keep.tile([P, S], U8, align_bytes=64)
+        nc.vector.tensor_copy(v_rows[:], tab_rows[:].indirect(gather_list[:]))
+        for q in range(QUADRANTS):
+            nc.sync.dma_start(
+                v_plane[q * QUADRANT : q * QUADRANT + SCALE_ROWS, :, :].bitcast(I32),
+                v_rows[q * QUADRANT_ROWS : (q + 1) * QUADRANT_ROWS, :].bitcast(I32),
+            )
+        nc.sync.dma_start(tab[1][:].bitcast(I32), tab_hbm[1])
+        nc.sync.dma_start(w1_raw[1][:], w1_rows[1])
+
+        v_words = {}
+
+        def gather_words(a):
+            for half in range(2):
+                words = ring.tile([P, HALF], U32, name="v", tag=f"v{2 * a + half}", align_bytes=64)
+                nc.vector.tensor_copy(words[:], tab[a][:].indirect(gather_list[:, entries(half * HALF, HALF)]))
+                v_words[a, half] = words
+
+        gather_words(0)
+        w2_codes = keep.tile([P, PASSES, PACK, P, 2], U8, align_bytes=64)
+        nc.vector.tensor_copy(
+            w2_codes[:],
+            w2[:].rearrange("p a (m t e) -> p a t m e", t=PACK, e=2),
         )
+        w2_dealt = keep.tile([P, PASSES, PACK, P], U8, align_bytes=64)
+        nc.vector.tensor_copy(w2_dealt[:], w2_plane[:].rearrange("p a (m t) -> p a t m", t=PACK))
 
-        w1_rows = w1.rearrange("(a p i) c -> a p i c", a=PASSES, i=PACK)
-        w1_first = ring.tile([P, PACK, H], F32, tag="w1_raw")
-        nc.sync.dma_start(w1_first[:], w1_rows[0])
-
-        v_plane = keep.tile([P, PASSES, S], U8, align_bytes=64)
-        w2_plane = keep.tile([P, PASSES, H], U8, align_bytes=64)
-        nc.vector.memset(w2_plane[:].bitcast(I32), 0)
-        load_scale_rows(nc.sync, w2_plane, w2_scales)
-        nc.vector.memset(v_plane[:].bitcast(I32), 0)
-        identity = keep.tile([P, P], F32)
-        make_identity(nc, identity[:])
-
-        tab = {}
-
-        def load_tab(a):
-            tab[a] = ring.tile([P, T], U32, name=f"tab{a}", tag=f"tab{a}")
-            nc.sync.dma_start(tab[a][:].bitcast(I32), tab_words[a].rearrange("p t i -> p (t i)").bitcast(I32))
-
-        load_tab(0)
 
         wgs_rows = wgs.rearrange("(m t) j -> m t j", t=PACK)
         page_rows = page0.rearrange("(p t) c -> t p c", t=PACK)
         out_rows = out_1.rearrange("(p t) c -> t p c", t=PACK)
 
-        v_rows = ring.tile([P, S], U8, tag="v_rows", align_bytes=64)
-        nc.vector.tensor_copy(v_rows[:], tab_rows[:].indirect(gather_list[:]))
-        for q in range(QUADRANTS):
-            nc.sync.dma_start(
-                v_plane[q * QUADRANT : q * QUADRANT + SCALE_ROWS, :, :].bitcast(I32),
-                v_rows[q * QUADRANT : (q + 1) * QUADRANT : ROW_STEP, :].bitcast(I32),
-            )
-
-        load_tab(1)
-
-        def gather_words(a, half, tag):
-            words = ring.tile([P, HALF], U32, name=tag, tag=tag, align_bytes=64)
-            nc.vector.tensor_copy(words[:], tab[a][:].indirect(gather_list[:, entries(half * HALF, HALF)]))
-            return words
-
-        w1_codes = [keep.tile([P, H], U32, name=f"w1_codes{a}", align_bytes=64) for a in range(PASSES)]
-        w1_plane = [keep.tile([P, H], U8, name=f"w1_plane{a}", align_bytes=64) for a in range(PASSES)]
-
-        def quantise_w1(a, c0, raw, tag):
-            width = raw.shape[2]
-            woven = ring.tile([P, width, PACK], BF16, name=tag, tag=tag, align_bytes=64)
-            nc.vector.tensor_copy(
-                woven[:].rearrange("p (c n) i -> p c i n", n=4), raw.rearrange("p i (c n) -> p c i n", n=4)
-            )
-            nc.vector.quantize_mx(
-                out=w1_codes[a][:, c0 : c0 + width].bitcast(E4M3X4),
-                scales=w1_plane[a][:, c0 : c0 + width],
-                in_=woven[:].rearrange("p c i -> p (c i)"),
-            )
-
-        quantise_w1(0, 0, w1_first[:], "w1a")
-        w1_second = ring.tile([P, 2, PACK, H // 2], F32, tag="w1_raw")
-        for u in range(2):
-            nc.sync.dma_start(w1_second[:, u], w1_rows[1][:, :, u * H // 2 : (u + 1) * H // 2])
-        v_words = {(a, half): gather_words(a, half, f"v{a}{half}") for a, half in ((0, 0), (0, 1), (1, 0))}
-        quantise_w1(1, 0, w1_second[:, 0], "w1b")
-        quantise_w1(1, H // 2, w1_second[:, 1], "last")
-        v_words[1, 1] = gather_words(1, 1, "last")
-
-        pages, weights = {}, {}
-
-        def load_page(t, tag):
-            pages[t] = ring.tile([P, T2], F32, name=f"page{t}", tag=tag, align_bytes=64)
-            nc.sync.dma_start(pages[t][:], page_rows[t])
-
-        def load_wgs(tile, slices, first):
+        def load_wgs(name, kib, slices, first, count):
+            tile = place(name, [P, len(slices), count], F32, kib)
             for q in (0, 2, 1, 3):
-                rows = wgs_rows[:, slices.start : slices.stop, first : first + tile.shape[2]]
+                rows = wgs_rows[:, slices.start : slices.stop, first : first + count]
                 nc.sync.dma_start(tile[q * QUADRANT : (q + 1) * QUADRANT], rows)
-            for t in slices:
-                weights[t, first] = tile[:, t - slices.start, :]
+            return {(t, first): tile[:, t - slices.start, :] for t in slices}
 
-        load_page(0, "v_rows")
-        early = ring.tile([P, 2, HALF], F32, tag="tab0")
-        load_wgs(early[:, 0:1, :], range(0, 1), 0)
-        load_wgs(early[:, 1:2, :], range(1, 2), 0)
-        load_page(1, "w1b")
-        middle = ring.tile([P, 2, HALF], F32, tag="w1_raw")
-        load_wgs(middle[:], range(0, 2), HALF)
-        late = ring.tile([P, 1, S], F32, tag="tab1")
-        load_wgs(late[:], range(2, 3), 0)
+        def load_page(t, kib):
+            page = place(f"page{t}", [P, T2], F32, kib)
+            nc.sync.dma_start(page[:], page_rows[t])
+            return page
 
-        def view(block, weight_codes, weight_plane, sign, tag):
-            half, c0 = divmod(block * P, HALF)
-            bank = psum.tile([P, H], F32, name="bank", tag="stage", bufs=STAGE_BANKS)
-            for a in range(PASSES):
-                nc.tensor.matmul_mx(
-                    out=bank[:],
-                    lhsT=v_words[a, half][:, c0 : c0 + P].bitcast(E4M3X4),
-                    lhsT_scale=v_plane[:, a, block * P : (block + 1) * P],
-                    rhs=weight_codes[a],
-                    rhs_scale=weight_plane[a],
-                    start=(a == 0),
-                    stop=(a == PASSES - 1),
+        pages = [load_page(0, 52)]
+        weights = load_wgs("wgs_first", 48, range(0, 1), 0, FIRST)
+        weights.update(load_wgs("wgs_rest", 49, range(0, 1), FIRST, S - FIRST))
+
+        w1_codes = [keep.tile([P, PACK, P], U32, name=f"w1_codes{a}", align_bytes=64) for a in range(PASSES)]
+        w1_plane = [keep.tile([P, PACK, P], U8, name=f"w1_plane{a}", align_bytes=64) for a in range(PASSES)]
+
+        def quantise_w1(a, slices, widths):
+            woven = ring.tile([P, len(slices), P, PACK], BF16, name="w1_woven", tag="w1_woven", align_bytes=64)
+            raw = w1_raw[a][:].rearrange("p i (m t) -> p m i t", t=PACK)[:, :, :, slices.start : slices.stop]
+            nc.vector.tensor_copy(woven[:].rearrange("p t m i -> p m i t"), raw)
+            t0 = 0
+            for width in widths:
+                there = slice(slices.start + t0, slices.start + t0 + width)
+                nc.vector.quantize_mx(
+                    out=w1_codes[a][:, there, :].rearrange("p t m -> p (t m)").bitcast(E4M3X4),
+                    scales=w1_plane[a][:, there, :].rearrange("p t m -> p (t m)"),
+                    in_=woven[:, t0 : t0 + width].rearrange("p t m i -> p (t m i)"),
                 )
-            tanh = ring.tile([P, PACK, P], F32, name=tag, tag=tag, bufs=BLOCKS)
-            nc.scalar.activation(tanh[:], bank[:].rearrange("p (m t) -> p t m", t=PACK), ACT.Tanh, scale=sign)
+                t0 = t0 + width
+
+        quantise_w1(0, range(0, PACK), (PACK,))
+        pages.append(load_page(1, 0))
+        gather_words(1)
+        weights.update(load_wgs("wgs_later", 28, range(1, PACK), 0, S))
+        pages.append(load_page(2, 16))
+        quantise_w1(1, range(0, 1), (1,))
+        quantise_w1(1, range(1, PACK), (1, 2))
+
+        pages.append(load_page(3, 8))
+        w3 = place("w3", [P, N], U32, 24)
+        nc.sync.dma_start(w3[:].bitcast(I32), w3_words[0].rearrange("p c i -> p (c i)").bitcast(I32))
+        w3_plane = place("w3_plane", [P, 1, N], U8, 27)
+        nc.gpsimd.memset(w3_plane[:].bitcast(I32), 0)
+        load_scale_rows(nc.sync, w3_plane, w3_scales)
+
+        def first_product(bank, first, codes, planes):
+            count = bank.shape[1]
+            for a in range(PASSES):
+                for c0 in range(0, count, P):
+                    half, c1 = divmod(first + c0, HALF)
+                    nc.tensor.matmul_mx(
+                        out=bank[:, c0 : c0 + P],
+                        lhsT=v_words[a, half][:, c1 : c1 + P].bitcast(E4M3X4),
+                        lhsT_scale=v_plane[:, a, first + c0 : first + c0 + P],
+                        rhs=codes[a],
+                        rhs_scale=planes[a],
+                        start=(a, c0) == (0, 0),
+                        stop=(a, c0) == (PASSES - 1, count - P),
+                    )
+
+        def view(t, first, count, number, codes, planes, sign, tag, bufs):
+            bank = new_bank(count, number)
+            first_product(bank[:], first, codes(t), planes(t))
+            tanh = ring.tile([P, count], F32, name=tag, tag=tag, bufs=bufs)
+            nc.scalar.activation(tanh[:], bank[:], ACT.Tanh, scale=sign)
             return tanh
 
-        w1_ops = [w1_codes[a][:].bitcast(E4M3X4) for a in range(PASSES)], [w1_plane[a][:] for a in range(PASSES)]
-        w2_ops = [w2[:, a, :].bitcast(E2M1X4) for a in range(PASSES)], [w2_plane[:, a, :] for a in range(PASSES)]
-        plus, minus = {}, {}
+        def w1_view(t, first, count, number):
+            return view(
+                t, first, count, number, lambda t: [w1_codes[a][:, t, :].bitcast(E4M3X4) for a in range(PASSES)],
+                lambda t: [w1_plane[a][:, t, :] for a in range(PASSES)], 1.0, "plus", 4,
+            )
 
-        def scatter(t, first, count):
-            h = ring.tile([P, count], F32, name="h", tag=f"h{t}_{first}", align_bytes=64)
-            for c0 in range(0, count, BANK):
-                width = min(count, BANK)
-                bank = psum.tile([P, width], F32, name="bank", tag="stage", bufs=STAGE_BANKS)
-                for b0 in range(0, width, P):
-                    block = (first + c0 + b0) // P
-                    for term, opens in ((minus[block], True), (plus[block], False)):
-                        nc.tensor.matmul(
-                            bank[:, b0 : b0 + P], lhsT=term[:, t, :], rhs=identity[:], is_transpose=True,
-                            start=opens, stop=not opens,
-                        )
-                if (t, first) == (0, 0):
-                    nc.vector.tensor_scalar(h[:], bank[:], gains[:, t : t + 1], None, ALU.mult)
-                else:
-                    nc.scalar.activation(h[:, c0 : c0 + width], bank[:], ACT.Copy, scale=gains[:, t : t + 1])
+        def w2_view(t, first, count, number):
+            return view(
+                t, first, count, number,
+                lambda t: [w2_codes[:, a, t].rearrange("p m e -> p (m e)").bitcast(E2M1X4) for a in range(PASSES)],
+                lambda t: [w2_dealt[:, a, t, :] for a in range(PASSES)], -1.0, "minus", BLOCKS,
+            )
+
+        def difference(h, t, minus, plus, number):
+            count = plus.shape[1]
+            bank = new_bank(count, number)
+            for u, term in enumerate((minus, plus)):
+                for c0 in range(0, count, P):
+                    nc.tensor.matmul(
+                        bank[:, c0 : c0 + P], lhsT=term[:, c0 : c0 + P], rhs=identity[:], is_transpose=True,
+                        start=(u, c0) == (0, 0), stop=(u, c0) == (1, count - P),
+                    )
+            nc.scalar.activation(h, bank[:], ACT.Copy, scale=gains[:, t : t + 1])
+
+        def scatter(t, first, h):
+            count = h.shape[1]
             w0 = max(c0 for s, c0 in weights if s == t and c0 <= first)
             nc.vector.tensor_tensor(
                 pages[t][:].indirect(scatter_list[:, entries(first, count)]),
-                h[:], weights[t, w0][:, first - w0 : first - w0 + count], ALU.mult,
+                h, weights[t, w0][:, first - w0 : first - w0 + count], ALU.mult,
             )
 
-        for h0 in range(0, S, HALF):
-            for block in range(h0 // P, (h0 + HALF) // P):
-                minus[block] = view(block, *w2_ops, -1.0, "minus")
-            for first in range(h0, h0 + HALF, QUARTER):
-                for block in range(first // P, (first + QUARTER) // P):
-                    plus[block] = view(block, *w1_ops, 1.0, "plus")
-                scatter(0, first, QUARTER)
-            scatter(1, h0, HALF)
-        load_page(2, "h0_0")
-        latest = ring.tile([P, 1, S], F32, tag=f"h0_{QUARTER}", align_bytes=64)
-        load_wgs(latest[:], range(3, PACK), 0)
-        load_page(3, "h1_0")
-        w3 = ring.tile([P, N], U32, tag=f"h0_{HALF}", align_bytes=64)
-        nc.sync.dma_start(w3[:].bitcast(I32), w3_words[0].rearrange("p c i -> p (c i)").bitcast(I32))
-        w3_plane = ring.tile([P, 1, N], U8, tag=f"h0_{HALF + QUARTER}", align_bytes=64)
-        nc.gpsimd.memset(w3_plane[:].bitcast(I32), 0)
-        load_scale_rows(nc.sync, w3_plane, w3_scales)
-        for t in range(2, PACK):
-            scatter(t, 0, S)
+        minus = w2_view(0, 0, HALF, 0)
+        plus = [w1_view(0, u * FIRST, FIRST, 1 + u) for u in range(2)]
+        for u in range(2):
+            h = keep.tile([P, FIRST], F32, name=f"h0_{u}", align_bytes=64)
+            difference(h[:], 0, minus[:, u * FIRST : (u + 1) * FIRST], plus[u][:], 3 + u)
+            scatter(0, u * FIRST, h[:])
+        h = keep.tile([P, HALF], F32, name="h0_2", align_bytes=64)
+        difference(h[:], 0, w2_view(0, HALF, HALF, 5)[:], w1_view(0, HALF, HALF, 6)[:], 1)
+        scatter(0, HALF, h[:])
+        for t in range(1, PACK):
+            h = keep.tile([P, S], F32, name=f"h{t}", align_bytes=64)
+            minus = [w2_view(t, u * HALF, HALF, VIEW_BANKS[(4 * t - 4 + u) % 5]) for u in range(2)]
+            plus = [w1_view(t, u * HALF, HALF, VIEW_BANKS[(4 * t - 2 + u) % 5]) for u in range(2)]
+            for u in range(2):
+                difference(h[:, u * HALF : (u + 1) * HALF], t, minus[u][:], plus[u][:], DIFFERENCE_BANKS[(2 * t - 2 + u) % 3])
+            scatter(t, 0, h[:])
 
-        pairs = [keep.tile([P, 2, BANK, 2], BF16, name=f"pairs{c}") for c in range(CHUNKS)]
+        pairs = [ring.tile([P, 2, BANK, 2], BF16, name="pairs", tag=f"v{c}", align_bytes=64) for c in range(CHUNKS)]
         for t in range(PACK):
             nc.sync.dma_start(out_rows[t], pages[t][:])
             for c in range(CHUNKS):
@@ -258,7 +282,6 @@ def tile_list_vault_retest_kernel(
         def store_codes(c0):
             nc.sync.dma_start(codes_out[:, c0 : c0 + span], page_codes[:, c0 : c0 + span].bitcast(I32))
 
-        banks = [("spare", BANKS - STAGE_BANKS)] * (BANKS - STAGE_BANKS) + [("stage", STAGE_BANKS)] * STAGE_BANKS
         for c0 in range(0, T2, span):
             quantise_page(c0)
             store_codes(c0)
@@ -272,9 +295,7 @@ def tile_list_vault_retest_kernel(
                 y = ring.tile([P, span], F32, name="y", tag="y", bufs=8)
                 for c1 in range(0, span, BANK):
                     cols = slice(c0 + c1, c0 + c1 + BANK)
-                    turn = (c0 // span * (N // P) + n0 // P) * STORE_CHUNKS + c1 // BANK
-                    tag, bufs = banks[turn % BANKS]
-                    e = psum.tile([P, BANK], F32, name="bank", tag=tag, bufs=bufs)
+                    e = new_bank(BANK, ((c0 // span * (N // P) + n0 // P) * STORE_CHUNKS + c1 // BANK) % BANKS)
                     nc.tensor.matmul_mx(
                         out=e[:],
                         lhsT=w3[:, n0 : n0 + P].bitcast(E4M3X4),

@@ -71,7 +71,7 @@ def tile_list_vault_retest_kernel(
         nc.vector.memset(w2_plane[:].bitcast(I32), 0)
         gather_list = keep.tile([P, S // LIST_ROWS], U16)
         nc.sync.dma_start(gather_list[:], offs)
-        tab_rows = place("tab_rows", [P, T], U8, 14)
+        tab_rows = place("tab_rows", [P, T], U8, 30)
         nc.sync.dma_start(
             tab_rows[:QUADRANT, :].bitcast(I32), tab_scales.rearrange("a q c -> q a c").bitcast(I32)
         )
@@ -89,7 +89,7 @@ def tile_list_vault_retest_kernel(
         identity = keep.tile([P, P], F32)
         make_identity(nc, identity[:])
         w1_rows = w1.rearrange("(a p i) c -> a p i c", a=PASSES, i=PACK)
-        w1_raw = [place(f"w1_raw{a}", [P, PACK, H], F32, 8 * a) for a in range(PASSES)]
+        w1_raw = [place(f"w1_raw{a}", [P, PACK, H], F32, 32 * a) for a in range(PASSES)]
         nc.sync.dma_start(w1_raw[0][:], w1_rows[0])
         scatter_list = keep.tile([P, S // LIST_ROWS], U16)
         nc.sync.dma_start(scatter_list[:], offs2)
@@ -147,32 +147,42 @@ def tile_list_vault_retest_kernel(
         w1_codes = [keep.tile([P, PACK, P], U32, name=f"w1_codes{a}", align_bytes=64) for a in range(PASSES)]
         w1_plane = [keep.tile([P, PACK, P], U8, name=f"w1_plane{a}", align_bytes=64) for a in range(PASSES)]
 
-        def quantise_w1(a, slices, widths):
-            woven = ring.tile([P, len(slices), P, PACK], BF16, name="w1_woven", tag="w1_woven", align_bytes=64)
-            raw = w1_raw[a][:].rearrange("p i (m t) -> p m i t", t=PACK)[:, :, :, slices.start : slices.stop]
-            nc.vector.tensor_copy(woven[:].rearrange("p t m i -> p m i t"), raw)
-            t0 = 0
-            for width in widths:
-                there = slice(slices.start + t0, slices.start + t0 + width)
-                nc.vector.quantize_mx(
-                    out=w1_codes[a][:, there, :].rearrange("p t m -> p (t m)").bitcast(E4M3X4),
-                    scales=w1_plane[a][:, there, :].rearrange("p t m -> p (t m)"),
-                    in_=woven[:, t0 : t0 + width].rearrange("p t m i -> p (t m i)"),
-                )
-                t0 = t0 + width
+        def quantise_w1(a, slices, dealt):
+            there = slice(slices.start, slices.stop)
+            nc.vector.quantize_mx(
+                out=w1_codes[a][:, there, :].rearrange("p t m -> p (t m)").bitcast(E4M3X4),
+                scales=w1_plane[a][:, there, :].rearrange("p t m -> p (t m)"),
+                in_=dealt.rearrange("p t m u -> p (t m u)").bitcast(BF16),
+            )
 
-        quantise_w1(0, range(0, PACK), (PACK,))
+        def weave_and_deal(a, slices):
+            woven = ring.tile([P, H, PACK], BF16, name="w1_woven", tag="w1_woven", align_bytes=64)
+            nc.vector.tensor_copy(
+                woven[:].rearrange("p (c n) i -> p c i n", n=4), w1_raw[a][:].rearrange("p i (c n) -> p c i n", n=4)
+            )
+            words = woven[:].rearrange("p c i -> p (c i)").bitcast(I32).rearrange("p (m t u) -> p t m u", t=PACK, u=2)
+            dealt = ring.tile([P, len(slices), P, 2], I32, name="w1_dealt", tag="w1_dealt", align_bytes=64)
+            nc.vector.tensor_copy(dealt[:], words[:, slices.start : slices.stop])
+            return dealt
+
+        quantise_w1(0, range(0, PACK), weave_and_deal(0, range(0, PACK))[:])
         pages.append(load_page(1, 0))
         gather_words(1)
-        weights.update(load_wgs("wgs_later", 28, range(1, PACK), 0, S))
+        weights.update(load_wgs("wgs1", 28, range(1, 2), 0, S))
         pages.append(load_page(2, 16))
-        quantise_w1(1, range(0, 1), (1,))
-        quantise_w1(1, range(1, PACK), (1, 2))
+        weights.update(load_wgs("wgs2", 24, range(2, 3), 0, S))
+        first = ring.tile([P, P, PACK], BF16, name="w1_woven", tag="w1_woven", align_bytes=64)
+        nc.vector.tensor_copy(first[:], w1_raw[1][:].rearrange("p i (m t) -> p m i t", t=PACK)[:, :, :, 0])
+        quantise_w1(1, range(0, 1), first[:].rearrange("p m i -> p (m i)").bitcast(I32).rearrange("p (t m u) -> p t m u", t=1, u=2))
+        dealt = weave_and_deal(1, range(1, PACK))
+        quantise_w1(1, range(1, 2), dealt[:, 0:1])
+        quantise_w1(1, range(2, PACK), dealt[:, 1:])
 
-        pages.append(load_page(3, 8))
-        w3 = place("w3", [P, N], U32, 24)
+        pages.append(load_page(3, 39.75))
+        weights.update(load_wgs("wgs3", 32, range(3, PACK), 0, S))
+        w3 = place("w3", [P, N], U32, 36)
         nc.sync.dma_start(w3[:].bitcast(I32), w3_words[0].rearrange("p c i -> p (c i)").bitcast(I32))
-        w3_plane = place("w3_plane", [P, 1, N], U8, 27)
+        w3_plane = place("w3_plane", [P, 1, N], U8, 39)
         nc.gpsimd.memset(w3_plane[:].bitcast(I32), 0)
         load_scale_rows(nc.sync, w3_plane, w3_scales)
 

@@ -33,17 +33,16 @@ QUADRANT_ROWS = PASSES * SCALE_ROWS
 BANKS = 8
 HALF = S // 2
 FIRST = 256
+HOLDS = (3, 2)
 VIEW_BANKS = (2, 3, 4, 6, 1)
 DIFFERENCE_BANKS = (0, 5, 7)
 KIB = 1024
 
 
 def load_scale_rows(queue, plane, scales):
-    for q in range(QUADRANTS):
-        rows = scales[:, q * SCALE_ROWS : (q + 1) * SCALE_ROWS, :].rearrange("a r c -> r a c")
-        queue.dma_start(
-            out=plane[q * QUADRANT : q * QUADRANT + SCALE_ROWS, :, :].bitcast(I32), in_=rows.bitcast(I32)
-        )
+    rows = scales.rearrange("a (q r) c -> r q a c", r=SCALE_ROWS)
+    for r in range(SCALE_ROWS):
+        queue.dma_start(out=plane[r:P:QUADRANT, :, :].bitcast(I32), in_=rows[r].bitcast(I32))
 
 
 def entries(first, count):
@@ -75,7 +74,7 @@ def tile_list_vault_retest_kernel(
         nc.sync.dma_start(
             tab_rows[:QUADRANT, :].bitcast(I32), tab_scales.rearrange("a q c -> q a c").bitcast(I32)
         )
-        nc.gpsimd.memset(tab_rows[QUADRANT : 2 * QUADRANT, :].bitcast(I32), 0)
+        nc.vector.memset(tab_rows[QUADRANT : 2 * QUADRANT, :].bitcast(I32), 0)
         nc.vector.memset(tab_rows[2 * QUADRANT :, :].bitcast(I32), 0)
         tab = [place("tab0", [P, T], U32, 48), place("tab1", [P, T], U32, 16)]
         tab_hbm = [tab_words[a].rearrange("p t i -> p (t i)").bitcast(I32) for a in range(PASSES)]
@@ -257,70 +256,83 @@ def tile_list_vault_retest_kernel(
                 difference(h[:, u * HALF : (u + 1) * HALF], t, minus[u][:], plus[u][:], DIFFERENCE_BANKS[(2 * t - 2 + u) % 3])
             scatter(t, 0, h[:])
 
-        pairs = [ring.tile([P, 2, BANK, 2], BF16, name="pairs", tag=f"v{c}", align_bytes=64) for c in range(CHUNKS)]
+        rounded = [ring.tile([P, PACK * BANK], BF16, name="rounded", tag=f"v{c}", align_bytes=64) for c in range(CHUNKS)]
         for t in range(PACK):
             nc.sync.dma_start(out_rows[t], pages[t][:])
             for c in range(CHUNKS):
                 rows = pages[t][:, c * BANK : (c + 1) * BANK]
-                if (c, t) == (0, PACK - 1):
-                    nc.vector.tensor_copy(pairs[c][:, t // 2, :, t % 2], rows)
-                elif (c, t) == (0, PACK - 2):
-                    nc.scalar.copy(pairs[c][:, t // 2, :, :], rows.unsqueeze(2).to_broadcast([P, BANK, 2]))
+                if c == 0:
+                    slots = rounded[c][:].rearrange("p (c u e) -> p u c e", u=2, e=2)[:, t // 2]
                 else:
-                    nc.scalar.copy(pairs[c][:, t // 2, :, t % 2], rows)
+                    slots = rounded[c][:].rearrange("p (u c e) -> p u c e", u=2, e=2)[:, t // 2]
+                if (c, t) == (0, PACK - 1):
+                    for c0 in range(0, BANK, BANK // 2):
+                        nc.vector.tensor_copy(slots[:, c0 : c0 + BANK // 2, 1], rows[:, c0 : c0 + BANK // 2])
+                elif (c, t) == (0, PACK - 2):
+                    nc.scalar.copy(slots, rows.unsqueeze(2).to_broadcast([P, BANK, 2]))
+                else:
+                    nc.scalar.copy(slots[:, :, t % 2], rows)
 
         page_codes = keep.tile([P, T2], U32, align_bytes=64)
         page_plane = keep.tile([P, T2], U8, align_bytes=64)
         codes_out = out_2[0].rearrange("p m t -> p (m t)").bitcast(I32)
         span = STORE_CHUNKS * BANK
 
-        def quantise_page(c0):
-            for c in range(c0 // BANK, (c0 + span) // BANK):
-                cols = slice(c * BANK, (c + 1) * BANK)
-                woven = ring.tile([P, BANK, 2], F32, name="woven", tag="woven", bufs=2, align_bytes=64)
-                words = pairs[c][:].rearrange("p u c e -> p u (c e)").bitcast(F32).rearrange("p u c -> p c u")
-                if c == CHUNKS - 1:
-                    nc.scalar.copy(woven[:], words)
-                else:
-                    nc.vector.tensor_copy(woven[:], words)
-                nc.vector.quantize_mx(
-                    out=page_codes[:, cols].bitcast(E4M3X4),
-                    scales=page_plane[:, cols],
-                    in_=woven[:].rearrange("p c u -> p (c u)").bitcast(BF16),
-                )
+        def quantise(c0, values):
+            cols = slice(c0, c0 + values.shape[1] // PACK)
+            nc.vector.quantize_mx(out=page_codes[:, cols].bitcast(E4M3X4), scales=page_plane[:, cols], in_=values)
+
+        def weave(c, tag):
+            woven = ring.tile([P, BANK, 2], U32, name="woven", tag=tag, align_bytes=64)
+            words = rounded[c][:].bitcast(U32).rearrange("p (u c) -> p c u", u=2)
+            if c == CHUNKS - 1:
+                nc.scalar.copy(woven[:], words)
+            else:
+                nc.vector.tensor_copy(woven[:].bitcast(I32), words.bitcast(I32))
+            return woven[:].rearrange("p c u -> p (c u)").bitcast(BF16)
 
         def store_codes(c0):
             nc.sync.dma_start(codes_out[:, c0 : c0 + span], page_codes[:, c0 : c0 + span].bitcast(I32))
 
-        for c0 in range(0, T2, span):
-            quantise_page(c0)
-            store_codes(c0)
-        for q in range(QUADRANTS):
-            nc.sync.dma_start(
-                out_3[0, q * SCALE_ROWS : (q + 1) * SCALE_ROWS, :].bitcast(I32),
-                page_plane[q * QUADRANT : q * QUADRANT + SCALE_ROWS, :].bitcast(I32),
-            )
-        for c0 in range(0, T2, span):
-            for n0 in range(0, N, P):
-                y = ring.tile([P, span], F32, name="y", tag="y", bufs=8)
-                for c1 in range(0, span, BANK):
-                    cols = slice(c0 + c1, c0 + c1 + BANK)
-                    e = new_bank(BANK, ((c0 // span * (N // P) + n0 // P) * STORE_CHUNKS + c1 // BANK) % BANKS)
-                    nc.tensor.matmul_mx(
-                        out=e[:],
-                        lhsT=w3[:, n0 : n0 + P].bitcast(E4M3X4),
-                        lhsT_scale=w3_plane[:, 0, n0 : n0 + P],
-                        rhs=page_codes[:, cols].bitcast(E4M3X4),
-                        rhs_scale=page_plane[:, cols],
-                        start=True,
-                        stop=True,
-                    )
+        def results(c0, n0):
+            y = ring.tile([P, span], F32, name="y", tag="y", bufs=8)
+            for c1 in range(0, span, BANK):
+                cols = slice(c0 + c1, c0 + c1 + BANK)
+                turn = (c0 // span * (N // P) + n0 // P) * STORE_CHUNKS + c1 // BANK
+                e = new_bank(BANK, turn % BANKS)
+                nc.tensor.matmul_mx(
+                    out=e[:],
+                    lhsT=w3[:, n0 : n0 + P].bitcast(E4M3X4),
+                    lhsT_scale=w3_plane[:, 0, n0 : n0 + P],
+                    rhs=page_codes[:, cols].bitcast(E4M3X4),
+                    rhs_scale=page_plane[:, cols],
+                    start=True,
+                    stop=True,
+                )
+                if turn in HOLDS:
+                    square = ring.tile([P, BANK], F32, name="square", tag=f"held{turn}", align_bytes=64)
+                else:
                     square = ring.tile([P, BANK], F32, name="minus", tag="minus", bufs=BLOCKS)
-                    nc.scalar.activation(square[:], e[:], ACT.Square)
-                    nc.vector.scalar_tensor_tensor(
-                        y[:, c1 : c1 + BANK], square[:], 1.0, e[:], ALU.add, ALU.mult
-                    )
-                    if (c0, n0) == (T2 - span, N - P):
-                        nc.sync.dma_start(out_0[n0 : n0 + P, cols], y[:, c1 : c1 + BANK])
-                if (c0, n0) != (T2 - span, N - P):
-                    nc.sync.dma_start(out_0[n0 : n0 + P, c0 : c0 + span], y[:])
+                nc.scalar.activation(square[:], e[:], ACT.Square)
+                nc.vector.scalar_tensor_tensor(y[:, c1 : c1 + BANK], square[:], 1.0, e[:], ALU.add, ALU.mult)
+                if (c0, n0) == (T2 - span, N - P):
+                    nc.sync.dma_start(out_0[n0 : n0 + P, cols], y[:, c1 : c1 + BANK])
+            if (c0, n0) != (T2 - span, N - P):
+                nc.sync.dma_start(out_0[n0 : n0 + P, c0 : c0 + span], y[:])
+
+        for c0 in range(0, BANK, BANK // 2):
+            quantise(c0, rounded[0][:, PACK * c0 : PACK * (c0 + BANK // 2)])
+        quantise(BANK, weave(1, "woven1"))
+        store_codes(0)
+        for n0 in range(0, N // 2, P):
+            results(0, n0)
+        for c, turn in zip(range(STORE_CHUNKS, CHUNKS), HOLDS):
+            quantise(c * BANK, weave(c, f"held{turn}"))
+        store_codes(span)
+        scales_out = out_3[0].rearrange("(q r) c -> r q c", r=SCALE_ROWS)
+        for r in range(SCALE_ROWS):
+            nc.sync.dma_start(scales_out[r].bitcast(I32), page_plane[r:P:QUADRANT, :].bitcast(I32))
+        for n0 in range(N // 2, N, P):
+            results(0, n0)
+        for n0 in range(0, N, P):
+            results(span, n0)

@@ -97,7 +97,7 @@ def tile_list_vault_retest_kernel(
 
         v_rows = keep.tile([P, S], U8, align_bytes=64)
         nc.vector.tensor_copy(v_rows[:], tab_rows[:].indirect(gather_list[:]))
-        for q in range(QUADRANTS):
+        for q in (0, 2, 1, 3):
             nc.sync.dma_start(
                 v_plane[q * QUADRANT : q * QUADRANT + SCALE_ROWS, :, :].bitcast(I32),
                 v_rows[q * QUADRANT_ROWS : (q + 1) * QUADRANT_ROWS, :].bitcast(I32),
@@ -181,9 +181,6 @@ def tile_list_vault_retest_kernel(
         weights.update(load_wgs("wgs3", 32, range(3, PACK), 0, S))
         w3 = place("w3", [P, N], U32, 36)
         nc.sync.dma_start(w3[:].bitcast(I32), w3_words[0].rearrange("p c i -> p (c i)").bitcast(I32))
-        w3_plane = place("w3_plane", [P, 1, N], U8, 39)
-        nc.gpsimd.memset(w3_plane[:].bitcast(I32), 0)
-        load_scale_rows(nc.sync, w3_plane, w3_scales)
 
         def first_product(bank, first, codes, planes):
             count = bank.shape[1]
@@ -203,7 +200,10 @@ def tile_list_vault_retest_kernel(
         def view(t, first, count, number, codes, planes, sign, tag, bufs):
             bank = new_bank(count, number)
             first_product(bank[:], first, codes(t), planes(t))
-            tanh = ring.tile([P, count], F32, name=tag, tag=tag, bufs=bufs)
+            if t == PACK - 2:
+                tanh = ring.tile([P, count], F32, name=tag, tag=f"{tag}{first}", align_bytes=64)
+            else:
+                tanh = ring.tile([P, count], F32, name=tag, tag=tag, bufs=bufs)
             nc.scalar.activation(tanh[:], bank[:], ACT.Tanh, scale=sign)
             return tanh
 
@@ -242,9 +242,12 @@ def tile_list_vault_retest_kernel(
         minus = w2_view(0, 0, HALF, 0)
         plus = [w1_view(0, u * FIRST, FIRST, 1 + u) for u in range(2)]
         for u in range(2):
-            h = keep.tile([P, FIRST], F32, name=f"h0_{u}", align_bytes=64)
+            h = ring.tile([P, FIRST], F32, name="h0", tag=f"h0_{u}", align_bytes=64)
             difference(h[:], 0, minus[:, u * FIRST : (u + 1) * FIRST], plus[u][:], 3 + u)
             scatter(0, u * FIRST, h[:])
+        w3_plane = ring.tile([P, 1, N], U8, name="w3_plane", tag="h0_0", align_bytes=64)
+        nc.gpsimd.memset(w3_plane[:].bitcast(I32), 0)
+        load_scale_rows(nc.sync, w3_plane, w3_scales)
         h = keep.tile([P, HALF], F32, name="h0_2", align_bytes=64)
         difference(h[:], 0, w2_view(0, HALF, HALF, 5)[:], w1_view(0, HALF, HALF, 6)[:], 1)
         scatter(0, HALF, h[:])
@@ -256,7 +259,11 @@ def tile_list_vault_retest_kernel(
                 difference(h[:, u * HALF : (u + 1) * HALF], t, minus[u][:], plus[u][:], DIFFERENCE_BANKS[(2 * t - 2 + u) % 3])
             scatter(t, 0, h[:])
 
-        rounded = [ring.tile([P, PACK * BANK], BF16, name="rounded", tag=f"v{c}", align_bytes=64) for c in range(CHUNKS)]
+        rounded = [
+            ring.tile([P, PACK * BANK], BF16, name="rounded", tag=f"{tag}{first}", align_bytes=64)
+            for first in (0, HALF)
+            for tag in ("minus", "plus")
+        ]
         for t in range(PACK):
             nc.sync.dma_start(out_rows[t], pages[t][:])
             for c in range(CHUNKS):

@@ -70,7 +70,7 @@ def tile_list_vault_retest_kernel(
         nc.vector.memset(w2_plane[:].bitcast(I32), 0)
         gather_list = keep.tile([P, S // LIST_ROWS], U16)
         nc.sync.dma_start(gather_list[:], offs)
-        tab_rows = place("tab_rows", [P, T], U8, 30)
+        tab_rows = place("tab_rows", [P, T], U8, 32)
         nc.sync.dma_start(
             tab_rows[:QUADRANT, :].bitcast(I32), tab_scales.rearrange("a q c -> q a c").bitcast(I32)
         )
@@ -78,22 +78,19 @@ def tile_list_vault_retest_kernel(
         nc.vector.memset(tab_rows[2 * QUADRANT :, :].bitcast(I32), 0)
         tab = [place("tab0", [P, T], U32, 48), place("tab1", [P, T], U32, 16)]
         tab_hbm = [tab_words[a].rearrange("p t i -> p (t i)").bitcast(I32) for a in range(PASSES)]
+        nc.sync.dma_start(tab[0][:].bitcast(I32), tab_hbm[0])
         w2 = keep.tile([P, PASSES, 2 * H], U8, align_bytes=64)
         nc.sync.dma_start(w2[:].bitcast(I32), w2_words.rearrange("a p c -> p a c").bitcast(I32))
 
         v_plane = keep.tile([P, PASSES, S], U8, align_bytes=64)
         load_scale_rows(nc.sync, w2_plane, w2_scales)
-        nc.sync.dma_start(tab[0][:].bitcast(I32), tab_hbm[0])
         nc.vector.memset(v_plane[:].bitcast(I32), 0)
-        identity = keep.tile([P, P], F32)
-        make_identity(nc, identity[:])
         w1_rows = w1.rearrange("(a p i) c -> a p i c", a=PASSES, i=PACK)
-        w1_raw = [place(f"w1_raw{a}", [P, PACK, H], F32, 32 * a) for a in range(PASSES)]
+        w1_raw = [place(f"w1_raw{a}", [P, PACK, H], F32, 33 * a) for a in range(PASSES)]
         nc.sync.dma_start(w1_raw[0][:], w1_rows[0])
         scatter_list = keep.tile([P, S // LIST_ROWS], U16)
         nc.sync.dma_start(scatter_list[:], offs2)
-        gains = keep.tile([P, PACK], F32)
-        nc.sync.dma_start(gains[:], gain.rearrange("(p t) -> p t", t=PACK))
+        nc.sync.dma_start(tab[1][:].bitcast(I32), tab_hbm[1])
 
         v_rows = keep.tile([P, S], U8, align_bytes=64)
         nc.vector.tensor_copy(v_rows[:], tab_rows[:].indirect(gather_list[:]))
@@ -102,8 +99,11 @@ def tile_list_vault_retest_kernel(
                 v_plane[q * QUADRANT : q * QUADRANT + SCALE_ROWS, :, :].bitcast(I32),
                 v_rows[q * QUADRANT_ROWS : (q + 1) * QUADRANT_ROWS, :].bitcast(I32),
             )
-        nc.sync.dma_start(tab[1][:].bitcast(I32), tab_hbm[1])
+        identity = place("identity", [P, P], F32, 32)
+        make_identity(nc, identity[:])
         nc.sync.dma_start(w1_raw[1][:], w1_rows[1])
+        gains = place("gains", [P, PACK], F32, 32.5)
+        nc.sync.dma_start(gains[:], gain.rearrange("(p t) -> p t", t=PACK))
 
         v_words = {}
 
@@ -177,9 +177,9 @@ def tile_list_vault_retest_kernel(
         quantise_w1(1, range(1, 2), dealt[:, 0:1])
         quantise_w1(1, range(2, PACK), dealt[:, 1:])
 
-        pages.append(load_page(3, 39.75))
-        weights.update(load_wgs("wgs3", 32, range(3, PACK), 0, S))
-        w3 = place("w3", [P, N], U32, 36)
+        pages.append(load_page(3, 40))
+        weights.update(load_wgs("wgs3", 33, range(3, PACK), 0, S))
+        w3 = place("w3", [P, N], U32, 37)
         nc.sync.dma_start(w3[:].bitcast(I32), w3_words[0].rearrange("p c i -> p (c i)").bitcast(I32))
 
         def first_product(bank, first, codes, planes):

@@ -322,10 +322,7 @@ def tile_list_vault_retest_kernel(
                     square = ring.tile([P, BANK], F32, name="minus", tag="minus", bufs=BLOCKS)
                 nc.scalar.activation(square[:], e[:], ACT.Square)
                 nc.vector.scalar_tensor_tensor(y[:, c1 : c1 + BANK], square[:], 1.0, e[:], ALU.add, ALU.mult)
-                if (c0, n0) == (T2 - span, N - P):
-                    nc.sync.dma_start(out_0[n0 : n0 + P, cols], y[:, c1 : c1 + BANK])
-            if (c0, n0) != (T2 - span, N - P):
-                nc.sync.dma_start(out_0[n0 : n0 + P, c0 : c0 + span], y[:])
+            nc.sync.dma_start(out_0[n0 : n0 + P, c0 : c0 + span], y[:])
 
         for c0 in range(0, BANK, BANK // 2):
             quantise(c0, rounded[0][:, PACK * c0 : PACK * (c0 + BANK // 2)])

@@ -74,6 +74,8 @@ def tile_list_vault_retest_kernel(
         nc.sync.dma_start(
             tab_rows[:QUADRANT, :].bitcast(I32), tab_scales.rearrange("a q c -> q a c").bitcast(I32)
         )
+        wgs_quarters = keep.tile([P, S // QUADRANTS], F32)
+        nc.sync.dma_start(wgs_quarters[:], wgs.rearrange("(m t) (h c) -> t m h c", t=PACK, h=QUADRANTS)[0])
         nc.vector.memset(tab_rows[QUADRANT : 2 * QUADRANT, :].bitcast(I32), 0)
         nc.vector.memset(tab_rows[2 * QUADRANT :, :].bitcast(I32), 0)
         tab = [place("tab0", [P, T], U32, 48), place("tab1", [P, T], U32, 16)]
@@ -140,8 +142,21 @@ def tile_list_vault_retest_kernel(
             return page
 
         pages = [load_page(0, 52)]
-        weights = load_wgs("wgs_first", 48, range(0, 1), 0, FIRST)
-        weights.update(load_wgs("wgs_rest", 49, range(0, 1), FIRST, S - FIRST))
+        turned = new_bank(2 * P, 7)
+        repeated = keep.tile([P, QUADRANTS, 2, QUADRANTS, QUADRANT], F32)
+        for b in range(2):
+            nc.tensor.transpose(turned[:, b * P : (b + 1) * P], wgs_quarters[:, b * P : (b + 1) * P], identity[:])
+        for b in range(2):
+            rows = turned[:, b * P : (b + 1) * P].rearrange("p (m h) -> p h m", h=QUADRANTS)
+            nc.scalar.copy(repeated[:, :, b], rows.unsqueeze(2).to_broadcast([P, QUADRANTS, QUADRANTS, QUADRANT]))
+        wgs0 = keep.tile([P, S], F32)
+        blocks = repeated[:].rearrange("p h b r m -> p (h b) (r m)")
+        for u in range(2):
+            bank = new_bank(HALF, 3 + u)
+            for c0 in range(0, HALF, P):
+                nc.tensor.transpose(bank[:, c0 : c0 + P], blocks[:, (u * HALF + c0) // P], identity[:])
+            nc.scalar.copy(wgs0[:, u * HALF : (u + 1) * HALF], bank[:])
+        weights = {(0, 0): wgs0[:]}
 
         w1_codes = [keep.tile([P, PACK, P], U32, name=f"w1_codes{a}", align_bytes=64) for a in range(PASSES)]
         w1_plane = [keep.tile([P, PACK, P], U8, name=f"w1_plane{a}", align_bytes=64) for a in range(PASSES)]
@@ -154,28 +169,36 @@ def tile_list_vault_retest_kernel(
                 in_=dealt.rearrange("p t m u -> p (t m u)").bitcast(BF16),
             )
 
-        def weave_and_deal(a, slices):
+        def weave_and_deal(a, slices, copy, word):
             woven = ring.tile([P, H, PACK], BF16, name="w1_woven", tag="w1_woven", align_bytes=64)
-            nc.vector.tensor_copy(
-                woven[:].rearrange("p (c n) i -> p c i n", n=4), w1_raw[a][:].rearrange("p i (c n) -> p c i n", n=4)
-            )
-            words = woven[:].rearrange("p c i -> p (c i)").bitcast(I32).rearrange("p (m t u) -> p t m u", t=PACK, u=2)
-            dealt = ring.tile([P, len(slices), P, 2], I32, name="w1_dealt", tag="w1_dealt", align_bytes=64)
-            nc.vector.tensor_copy(dealt[:], words[:, slices.start : slices.stop])
+            copy(woven[:].rearrange("p (c n) i -> p c i n", n=4), w1_raw[a][:].rearrange("p i (c n) -> p c i n", n=4))
+            words = woven[:].rearrange("p c i -> p (c i)").bitcast(word).rearrange("p (m t u) -> p t m u", t=PACK, u=2)
+            dealt = ring.tile([P, len(slices), P, 2], word, name="w1_dealt", tag="w1_dealt", align_bytes=64)
+            copy(dealt[:], words[:, slices.start : slices.stop])
             return dealt
 
-        quantise_w1(0, range(0, PACK), weave_and_deal(0, range(0, PACK))[:])
+        quantise_w1(0, range(0, PACK), weave_and_deal(0, range(0, PACK), nc.vector.tensor_copy, I32)[:])
         pages.append(load_page(1, 0))
         gather_words(1)
         weights.update(load_wgs("wgs1", 28, range(1, 2), 0, S))
         pages.append(load_page(2, 16))
         weights.update(load_wgs("wgs2", 24, range(2, 3), 0, S))
-        first = ring.tile([P, P, PACK], BF16, name="w1_woven", tag="w1_woven", align_bytes=64)
+        first = keep.tile([P, P, PACK], BF16, align_bytes=64)
         nc.vector.tensor_copy(first[:], w1_raw[1][:].rearrange("p i (m t) -> p m i t", t=PACK)[:, :, :, 0])
         quantise_w1(1, range(0, 1), first[:].rearrange("p m i -> p (m i)").bitcast(I32).rearrange("p (t m u) -> p t m u", t=1, u=2))
-        dealt = weave_and_deal(1, range(1, PACK))
-        quantise_w1(1, range(1, 2), dealt[:, 0:1])
-        quantise_w1(1, range(2, PACK), dealt[:, 1:])
+        woven = keep.tile([P, H, PACK], BF16, align_bytes=64)
+        for c0, c1 in ((0, P), (P, H)):
+            nc.vector.tensor_copy(
+                woven[:, c0:c1].rearrange("p (c n) i -> p c i n", n=4),
+                w1_raw[1][:, :, c0:c1].rearrange("p i (c n) -> p c i n", n=4),
+            )
+        words = woven[:].rearrange("p c i -> p (c i)").bitcast(I32).rearrange("p (m t u) -> p t m u", t=PACK, u=2)
+        groups = (range(1, 2), range(2, PACK))
+        dealt = [keep.tile([P, len(g), P, 2], I32, name=f"dealt{g.start}", align_bytes=64) for g in groups]
+        for g, tile in zip(groups, dealt):
+            nc.vector.tensor_copy(tile[:], words[:, g.start : g.stop])
+        for g, tile in zip(groups, dealt):
+            quantise_w1(1, g, tile[:])
 
         pages.append(load_page(3, 40))
         weights.update(load_wgs("wgs3", 33, range(3, PACK), 0, S))
@@ -200,7 +223,7 @@ def tile_list_vault_retest_kernel(
         def view(t, first, count, number, codes, planes, sign, tag, bufs):
             bank = new_bank(count, number)
             first_product(bank[:], first, codes(t), planes(t))
-            if t == PACK - 2:
+            if t == PACK - 1:
                 tanh = ring.tile([P, count], F32, name=tag, tag=f"{tag}{first}", align_bytes=64)
             else:
                 tanh = ring.tile([P, count], F32, name=tag, tag=tag, bufs=bufs)

@@ -33,10 +33,13 @@ QUADRANT_ROWS = PASSES * SCALE_ROWS
 BANKS = 8
 HALF = S // 2
 FIRST = 256
-HOLDS = (3, 2)
+HOLD = 5
+SHARED = 64
+QUARTER = 256
 VIEW_BANKS = (2, 3, 4, 6, 1)
 DIFFERENCE_BANKS = (0, 5, 7)
 KIB = 1024
+ROUNDED = 70
 
 
 def load_scale_rows(queue, plane, scales):
@@ -178,9 +181,9 @@ def tile_list_vault_retest_kernel(
             return dealt
 
         quantise_w1(0, range(0, PACK), weave_and_deal(0, range(0, PACK), nc.vector.tensor_copy, I32)[:])
-        pages.append(load_page(1, 0))
         gather_words(1)
-        weights.update(load_wgs("wgs1", 28, range(1, 2), 0, S))
+        weights.update(load_wgs("wgs1", 48, range(1, 2), 0, S))
+        pages.append(load_page(1, 0))
         pages.append(load_page(2, 16))
         weights.update(load_wgs("wgs2", 24, range(2, 3), 0, S))
         first = keep.tile([P, P, PACK], BF16, align_bytes=64)
@@ -194,15 +197,15 @@ def tile_list_vault_retest_kernel(
             )
         words = woven[:].rearrange("p c i -> p (c i)").bitcast(I32).rearrange("p (m t u) -> p t m u", t=PACK, u=2)
         groups = (range(1, 2), range(2, PACK))
-        dealt = [keep.tile([P, len(g), P, 2], I32, name=f"dealt{g.start}", align_bytes=64) for g in groups]
+        dealt = [ring.tile([P, len(g), P, 2], I32, name="dealt", tag=f"dealt{g.start}", align_bytes=64) for g in groups]
         for g, tile in zip(groups, dealt):
             nc.vector.tensor_copy(tile[:], words[:, g.start : g.stop])
         for g, tile in zip(groups, dealt):
             quantise_w1(1, g, tile[:])
 
-        pages.append(load_page(3, 40))
-        weights.update(load_wgs("wgs3", 33, range(3, PACK), 0, S))
-        w3 = place("w3", [P, N], U32, 37)
+        pages.append(load_page(3, 33))
+        weights.update(load_wgs("wgs3", 60, range(3, PACK), 0, S))
+        w3 = place("w3", [P, N], U32, 28)
         nc.sync.dma_start(w3[:].bitcast(I32), w3_words[0].rearrange("p c i -> p (c i)").bitcast(I32))
 
         def first_product(bank, first, codes, planes):
@@ -223,8 +226,8 @@ def tile_list_vault_retest_kernel(
         def view(t, first, count, number, codes, planes, sign, tag, bufs):
             bank = new_bank(count, number)
             first_product(bank[:], first, codes(t), planes(t))
-            if t == PACK - 1:
-                tanh = ring.tile([P, count], F32, name=tag, tag=f"{tag}{first}", align_bytes=64)
+            if (t, first, tag) == (PACK - 1, HALF, "plus"):
+                tanh = place("last_plus", [P, 7 * count], F32, ROUNDED)[:, :count]
             else:
                 tanh = ring.tile([P, count], F32, name=tag, tag=tag, bufs=bufs)
             nc.scalar.activation(tanh[:], bank[:], ACT.Tanh, scale=sign)
@@ -243,7 +246,7 @@ def tile_list_vault_retest_kernel(
                 lambda t: [w2_dealt[:, a, t, :] for a in range(PASSES)], -1.0, "minus", BLOCKS,
             )
 
-        def difference(h, t, minus, plus, number):
+        def difference(h, t, first, minus, plus, number):
             count = plus.shape[1]
             bank = new_bank(count, number)
             for u, term in enumerate((minus, plus)):
@@ -252,114 +255,120 @@ def tile_list_vault_retest_kernel(
                         bank[:, c0 : c0 + P], lhsT=term[:, c0 : c0 + P], rhs=identity[:], is_transpose=True,
                         start=(u, c0) == (0, 0), stop=(u, c0) == (1, count - P),
                     )
-            nc.scalar.activation(h, bank[:], ACT.Copy, scale=gains[:, t : t + 1])
+            gain_t, wgs_t = gains[:, t : t + 1], weights[t, 0][:, first : first + count]
+            if (t, first) == (0, 0):
+                nc.vector.scalar_tensor_tensor(h, bank[:], gain_t, wgs_t, ALU.mult, ALU.mult)
+            else:
+                nc.scalar.activation(h, bank[:], ACT.Copy, scale=gain_t)
+                nc.gpsimd.tensor_tensor(h, h, wgs_t, ALU.mult)
 
         def scatter(t, first, h):
-            count = h.shape[1]
-            w0 = max(c0 for s, c0 in weights if s == t and c0 <= first)
-            nc.vector.tensor_tensor(
-                pages[t][:].indirect(scatter_list[:, entries(first, count)]),
-                h, weights[t, w0][:, first - w0 : first - w0 + count], ALU.mult,
-            )
+            nc.vector.tensor_copy(pages[t][:].indirect(scatter_list[:, entries(first, h.shape[1])]), h)
 
         minus = w2_view(0, 0, HALF, 0)
         plus = [w1_view(0, u * FIRST, FIRST, 1 + u) for u in range(2)]
         for u in range(2):
             h = ring.tile([P, FIRST], F32, name="h0", tag=f"h0_{u}", align_bytes=64)
-            difference(h[:], 0, minus[:, u * FIRST : (u + 1) * FIRST], plus[u][:], 3 + u)
+            difference(h[:], 0, u * FIRST, minus[:, u * FIRST : (u + 1) * FIRST], plus[u][:], 3 + u)
             scatter(0, u * FIRST, h[:])
-        w3_plane = ring.tile([P, 1, N], U8, name="w3_plane", tag="h0_0", align_bytes=64)
+        h = ring.tile([P, HALF], F32, name="h0", tag="h0_2", align_bytes=64)
+        difference(h[:], 0, HALF, w2_view(0, HALF, HALF, 5)[:], w1_view(0, HALF, HALF, 6)[:], 1)
+        scatter(0, HALF, h[:])
+        w3_plane = ring.tile([P, 1, N], U8, name="w3_plane", tag="dealt2", align_bytes=64)
         nc.gpsimd.memset(w3_plane[:].bitcast(I32), 0)
         load_scale_rows(nc.sync, w3_plane, w3_scales)
-        h = keep.tile([P, HALF], F32, name="h0_2", align_bytes=64)
-        difference(h[:], 0, w2_view(0, HALF, HALF, 5)[:], w1_view(0, HALF, HALF, 6)[:], 1)
-        scatter(0, HALF, h[:])
         for t in range(1, PACK):
             h = keep.tile([P, S], F32, name=f"h{t}", align_bytes=64)
             minus = [w2_view(t, u * HALF, HALF, VIEW_BANKS[(4 * t - 4 + u) % 5]) for u in range(2)]
             plus = [w1_view(t, u * HALF, HALF, VIEW_BANKS[(4 * t - 2 + u) % 5]) for u in range(2)]
             for u in range(2):
-                difference(h[:, u * HALF : (u + 1) * HALF], t, minus[u][:], plus[u][:], DIFFERENCE_BANKS[(2 * t - 2 + u) % 3])
+                difference(h[:, u * HALF : (u + 1) * HALF], t, u * HALF, minus[u][:], plus[u][:], DIFFERENCE_BANKS[(2 * t - 2 + u) % 3])
             scatter(t, 0, h[:])
 
-        rounded = [
-            ring.tile([P, PACK * BANK], BF16, name="rounded", tag=f"{tag}{first}", align_bytes=64)
-            for first in (0, HALF)
-            for tag in ("minus", "plus")
-        ]
+        span = STORE_CHUNKS * BANK
+        last = PACK - 1
+        flat = place("flat", [P, 2, T2], BF16, ROUNDED)
+        early = [place(f"early{k}", [P, QUARTER, PACK], BF16, ROUNDED + 8 + 2 * k)[:] for k in range(3)]
+        joined = place("joined", [P, QUARTER - SHARED + span, PACK], BF16, 60)
+        early.append(joined[:, :QUARTER])
+        late = joined[:, QUARTER - SHARED :]
+        quarters = [slice(c0, c0 + QUARTER) for c0 in range(0, span, QUARTER)]
+
+        def round_on_gpsimd(out, rows):
+            nc.gpsimd.tensor_scalar(out, rows, 1.0, 0.0, ALU.mult, ALU.add)
+
+        def twice(rows):
+            return rows.unsqueeze(2).to_broadcast([P, rows.shape[1], 2])
+
         for t in range(PACK):
             nc.sync.dma_start(out_rows[t], pages[t][:])
-            for c in range(CHUNKS):
-                rows = pages[t][:, c * BANK : (c + 1) * BANK]
-                if c == 0:
-                    slots = rounded[c][:].rearrange("p (c u e) -> p u c e", u=2, e=2)[:, t // 2]
-                else:
-                    slots = rounded[c][:].rearrange("p (u c e) -> p u c e", u=2, e=2)[:, t // 2]
-                if (c, t) == (0, PACK - 1):
-                    for c0 in range(0, BANK, BANK // 2):
-                        nc.vector.tensor_copy(slots[:, c0 : c0 + BANK // 2, 1], rows[:, c0 : c0 + BANK // 2])
-                elif (c, t) == (0, PACK - 2):
-                    nc.scalar.copy(slots, rows.unsqueeze(2).to_broadcast([P, BANK, 2]))
-                else:
-                    nc.scalar.copy(slots[:, :, t % 2], rows)
+        for t in range(2):
+            nc.scalar.copy(flat[:, t], pages[t][:])
+        for k, cols in enumerate(quarters):
+            nc.scalar.copy(early[k][:, :, :2], flat[:, :, cols].rearrange("p t c -> p c t"))
+        round_on_gpsimd(late[:, SHARED:, :2], flat[:, :, span + SHARED :].rearrange("p t c -> p c t"))
+        round_on_gpsimd(late[:, SHARED:, 2], pages[2][:, span + SHARED :])
+        for k, cols in enumerate(quarters):
+            if k < 2:
+                nc.scalar.copy(early[k][:, :, 2:], twice(pages[2][:, cols]))
+            else:
+                nc.scalar.copy(early[k][:, :, 2], pages[2][:, cols])
+        for k, cols in enumerate(quarters):
+            copy = nc.vector.tensor_copy if k < 2 else nc.scalar.copy
+            copy(early[k][:, :, last], pages[last][:, cols])
 
-        page_codes = keep.tile([P, T2], U32, align_bytes=64)
+        page_codes = {0: keep.tile([P, span], U32, name="early_codes", align_bytes=64)}
         page_plane = keep.tile([P, T2], U8, align_bytes=64)
         codes_out = out_2[0].rearrange("p m t -> p (m t)").bitcast(I32)
-        span = STORE_CHUNKS * BANK
 
         def quantise(c0, values):
-            cols = slice(c0, c0 + values.shape[1] // PACK)
-            nc.vector.quantize_mx(out=page_codes[:, cols].bitcast(E4M3X4), scales=page_plane[:, cols], in_=values)
-
-        def weave(c, tag):
-            woven = ring.tile([P, BANK, 2], U32, name="woven", tag=tag, align_bytes=64)
-            words = rounded[c][:].bitcast(U32).rearrange("p (u c) -> p c u", u=2)
-            if c == CHUNKS - 1:
-                nc.scalar.copy(woven[:], words)
-            else:
-                nc.vector.tensor_copy(woven[:].bitcast(I32), words.bitcast(I32))
-            return woven[:].rearrange("p c u -> p (c u)").bitcast(BF16)
+            count = values.shape[1] // PACK
+            codes = page_codes[c0 // span * span][:, c0 % span : c0 % span + count]
+            nc.vector.quantize_mx(out=codes.bitcast(E4M3X4), scales=page_plane[:, c0 : c0 + count], in_=values)
 
         def store_codes(c0):
-            nc.sync.dma_start(codes_out[:, c0 : c0 + span], page_codes[:, c0 : c0 + span].bitcast(I32))
+            nc.sync.dma_start(codes_out[:, c0 : c0 + span], page_codes[c0][:].bitcast(I32))
 
-        def results(c0, n0):
+        turns = []
+
+        def results(c0, n0, width):
             y = ring.tile([P, span], F32, name="y", tag="y", bufs=8)
-            for c1 in range(0, span, BANK):
-                cols = slice(c0 + c1, c0 + c1 + BANK)
-                turn = (c0 // span * (N // P) + n0 // P) * STORE_CHUNKS + c1 // BANK
-                e = new_bank(BANK, turn % BANKS)
+            for c1 in range(0, span, width):
+                e = new_bank(width, len(turns) % BANKS)
+                turns.append(c1)
                 nc.tensor.matmul_mx(
                     out=e[:],
                     lhsT=w3[:, n0 : n0 + P].bitcast(E4M3X4),
                     lhsT_scale=w3_plane[:, 0, n0 : n0 + P],
-                    rhs=page_codes[:, cols].bitcast(E4M3X4),
-                    rhs_scale=page_plane[:, cols],
+                    rhs=page_codes[c0][:, c1 : c1 + width].bitcast(E4M3X4),
+                    rhs_scale=page_plane[:, c0 + c1 : c0 + c1 + width],
                     start=True,
                     stop=True,
                 )
-                if turn in HOLDS:
-                    square = ring.tile([P, BANK], F32, name="square", tag=f"held{turn}", align_bytes=64)
+                if (c0, STORE_CHUNKS * n0 // P + c1 // BANK) == (0, HOLD):
+                    square = ring.tile([P, width], F32, name="square", tag="held", align_bytes=64)
                 else:
-                    square = ring.tile([P, BANK], F32, name="minus", tag="minus", bufs=BLOCKS)
+                    square = ring.tile([P, width], F32, name="minus", tag="minus", bufs=BLOCKS)
                 nc.scalar.activation(square[:], e[:], ACT.Square)
-                nc.vector.scalar_tensor_tensor(y[:, c1 : c1 + BANK], square[:], 1.0, e[:], ALU.add, ALU.mult)
+                nc.vector.scalar_tensor_tensor(y[:, c1 : c1 + width], square[:], 1.0, e[:], ALU.add, ALU.mult)
             nc.sync.dma_start(out_0[n0 : n0 + P, c0 : c0 + span], y[:])
 
-        for c0 in range(0, BANK, BANK // 2):
-            quantise(c0, rounded[0][:, PACK * c0 : PACK * (c0 + BANK // 2)])
-        quantise(BANK, weave(1, "woven1"))
+        for k, cols in enumerate(quarters):
+            quantise(cols.start, early[k].rearrange("p c t -> p (c t)"))
         store_codes(0)
-        for n0 in range(0, N // 2, P):
-            results(0, n0)
-        for c, turn in zip(range(STORE_CHUNKS, CHUNKS), HOLDS):
-            quantise(c * BANK, weave(c, f"held{turn}"))
+        round_on_gpsimd(late[:, :, last], pages[last][:, span:])
+        round_on_gpsimd(late[:, :SHARED, :2], flat[:, :, span : span + SHARED].rearrange("p t c -> p c t"))
+        round_on_gpsimd(late[:, :SHARED, 2], pages[2][:, span : span + SHARED])
+        results(0, 0, QUARTER)
+        for n0 in range(P, (HOLD // 2 + 1) * P, P):
+            results(0, n0, BANK)
+        page_codes[span] = ring.tile([P, span], U32, name="late_codes", tag="held", align_bytes=64)
+        quantise(span, late.rearrange("p c t -> p (c t)"))
         store_codes(span)
         scales_out = out_3[0].rearrange("(q r) c -> r q c", r=SCALE_ROWS)
         for r in range(SCALE_ROWS):
             nc.sync.dma_start(scales_out[r].bitcast(I32), page_plane[r:P:QUADRANT, :].bitcast(I32))
-        for n0 in range(N // 2, N, P):
-            results(0, n0)
+        for n0 in range((HOLD // 2 + 1) * P, N, P):
+            results(0, n0, BANK)
         for n0 in range(0, N, P):
-            results(span, n0)
+            results(span, n0, BANK)

from contextlib import ExitStack

import concourse.mybir as mybir
from concourse.masks import make_identity

K, H, N, T, S, T2 = 1024, 512, 768, 4096, 1024, 2048
FLOPS = 2 * 2 * K * H * S + 2 * H * N * T2

F32 = mybir.dt.float32
BF16 = mybir.dt.bfloat16
I32 = mybir.dt.int32
U32 = mybir.dt.uint32
U16 = mybir.dt.uint16
U8 = mybir.dt.uint8
E4M3X4 = mybir.dt.float8_e4m3fn_x4
E2M1X4 = mybir.dt.float4_e2m1fn_x4
ACT = mybir.ActivationFunctionType
ALU = mybir.AluOpType

P = 128
PACK = 4
K_PASS = P * PACK
PASSES = K // K_PASS
QUADRANTS = 4
QUADRANT = P // QUADRANTS
SCALE_ROWS = 4
LIST_ROWS = 16
BANK = 512
BLOCKS = S // P
CHUNKS = T2 // BANK
STORE_CHUNKS = 2
QUADRANT_ROWS = PASSES * SCALE_ROWS
BANKS = 8
HALF = S // 2
FIRST = 256
HOLD = 5
SHARED = 64
QUARTER = 256
VIEW_BANKS = (2, 3, 4, 6, 1)
DIFFERENCE_BANKS = (0, 5, 7)
KIB = 1024
ROUNDED = 70


def load_scale_rows(queue, plane, scales):
    rows = scales.rearrange("a (q r) c -> r q a c", r=SCALE_ROWS)
    for r in range(SCALE_ROWS):
        queue.dma_start(out=plane[r:P:QUADRANT, :, :].bitcast(I32), in_=rows[r].bitcast(I32))


def entries(first, count):
    return slice(first // LIST_ROWS, (first + count) // LIST_ROWS)


def tile_list_vault_retest_kernel(
    tc, tab_words, tab_scales, offs, w1, w2_words, w2_scales, gain, wgs, offs2, page0, w3_words, w3_scales,
    out_0, out_1, out_2, out_3,
):
    nc = tc.nc
    with ExitStack() as ctx:
        keep = ctx.enter_context(tc.tile_pool(name="keep", bufs=1))
        ring = ctx.enter_context(tc.tile_pool(name="ring", bufs=1))
        laid = ctx.enter_context(tc.tile_pool(name="laid", bufs=1))
        psum = ctx.enter_context(tc.psum_pool(name="psum", bufs=1))

        def place(name, shape, dtype, kib):
            return laid.tile(shape, dtype, name=name, offset=int(kib * KIB), align_bytes=64)

        def new_bank(width, number):
            return psum.tile([P, width], F32, name="bank", tag=f"bank{number}")

        w2_plane = keep.tile([P, PASSES, H], U8, align_bytes=64)
        nc.vector.memset(w2_plane[:].bitcast(I32), 0)
        gather_list = keep.tile([P, S // LIST_ROWS], U16)
        nc.sync.dma_start(gather_list[:], offs)
        tab_rows = place("tab_rows", [P, T], U8, 32)
        nc.sync.dma_start(
            tab_rows[:QUADRANT, :].bitcast(I32), tab_scales.rearrange("a q c -> q a c").bitcast(I32)
        )
        wgs_quarters = keep.tile([P, S // QUADRANTS], F32)
        nc.sync.dma_start(wgs_quarters[:], wgs.rearrange("(m t) (h c) -> t m h c", t=PACK, h=QUADRANTS)[0])
        nc.vector.memset(tab_rows[QUADRANT : 2 * QUADRANT, :].bitcast(I32), 0)
        nc.vector.memset(tab_rows[2 * QUADRANT :, :].bitcast(I32), 0)
        tab = [place("tab0", [P, T], U32, 48), place("tab1", [P, T], U32, 16)]
        tab_hbm = [tab_words[a].rearrange("p t i -> p (t i)").bitcast(I32) for a in range(PASSES)]
        nc.sync.dma_start(tab[0][:].bitcast(I32), tab_hbm[0])
        w2 = keep.tile([P, PASSES, 2 * H], U8, align_bytes=64)
        nc.sync.dma_start(w2[:].bitcast(I32), w2_words.rearrange("a p c -> p a c").bitcast(I32))

        v_plane = keep.tile([P, PASSES, S], U8, align_bytes=64)
        load_scale_rows(nc.sync, w2_plane, w2_scales)
        nc.vector.memset(v_plane[:].bitcast(I32), 0)
        w1_rows = w1.rearrange("(a p i) c -> a p i c", a=PASSES, i=PACK)
        w1_raw = [place(f"w1_raw{a}", [P, PACK, H], F32, 33 * a) for a in range(PASSES)]
        nc.sync.dma_start(w1_raw[0][:], w1_rows[0])
        scatter_list = keep.tile([P, S // LIST_ROWS], U16)
        nc.sync.dma_start(scatter_list[:], offs2)
        nc.sync.dma_start(tab[1][:].bitcast(I32), tab_hbm[1])

        v_rows = keep.tile([P, S], U8, align_bytes=64)
        nc.vector.tensor_copy(v_rows[:], tab_rows[:].indirect(gather_list[:]))
        for q in (0, 2, 1, 3):
            nc.sync.dma_start(
                v_plane[q * QUADRANT : q * QUADRANT + SCALE_ROWS, :, :].bitcast(I32),
                v_rows[q * QUADRANT_ROWS : (q + 1) * QUADRANT_ROWS, :].bitcast(I32),
            )
        identity = place("identity", [P, P], F32, 32)
        make_identity(nc, identity[:])
        nc.sync.dma_start(w1_raw[1][:], w1_rows[1])
        gains = place("gains", [P, PACK], F32, 32.5)
        nc.sync.dma_start(gains[:], gain.rearrange("(p t) -> p t", t=PACK))

        v_words = {}

        def gather_words(a):
            for half in range(2):
                words = ring.tile([P, HALF], U32, name="v", tag=f"v{2 * a + half}", align_bytes=64)
                nc.vector.tensor_copy(words[:], tab[a][:].indirect(gather_list[:, entries(half * HALF, HALF)]))
                v_words[a, half] = words

        gather_words(0)
        w2_codes = keep.tile([P, PASSES, PACK, P, 2], U8, align_bytes=64)
        nc.vector.tensor_copy(
            w2_codes[:],
            w2[:].rearrange("p a (m t e) -> p a t m e", t=PACK, e=2),
        )
        w2_dealt = keep.tile([P, PASSES, PACK, P], U8, align_bytes=64)
        nc.vector.tensor_copy(w2_dealt[:], w2_plane[:].rearrange("p a (m t) -> p a t m", t=PACK))


        wgs_rows = wgs.rearrange("(m t) j -> m t j", t=PACK)
        page_rows = page0.rearrange("(p t) c -> t p c", t=PACK)
        out_rows = out_1.rearrange("(p t) c -> t p c", t=PACK)

        def load_wgs(name, kib, slices, first, count):
            tile = place(name, [P, len(slices), count], F32, kib)
            for q in (0, 2, 1, 3):
                rows = wgs_rows[:, slices.start : slices.stop, first : first + count]
                nc.sync.dma_start(tile[q * QUADRANT : (q + 1) * QUADRANT], rows)
            return {(t, first): tile[:, t - slices.start, :] for t in slices}

        def load_page(t, kib):
            page = place(f"page{t}", [P, T2], F32, kib)
            nc.sync.dma_start(page[:], page_rows[t])
            return page

        pages = [load_page(0, 52)]
        turned = new_bank(2 * P, 7)
        repeated = keep.tile([P, QUADRANTS, 2, QUADRANTS, QUADRANT], F32)
        for b in range(2):
            nc.tensor.transpose(turned[:, b * P : (b + 1) * P], wgs_quarters[:, b * P : (b + 1) * P], identity[:])
        for b in range(2):
            rows = turned[:, b * P : (b + 1) * P].rearrange("p (m h) -> p h m", h=QUADRANTS)
            nc.scalar.copy(repeated[:, :, b], rows.unsqueeze(2).to_broadcast([P, QUADRANTS, QUADRANTS, QUADRANT]))
        wgs0 = keep.tile([P, S], F32)
        blocks = repeated[:].rearrange("p h b r m -> p (h b) (r m)")
        for u in range(2):
            bank = new_bank(HALF, 3 + u)
            for c0 in range(0, HALF, P):
                nc.tensor.transpose(bank[:, c0 : c0 + P], blocks[:, (u * HALF + c0) // P], identity[:])
            nc.scalar.copy(wgs0[:, u * HALF : (u + 1) * HALF], bank[:])
        weights = {(0, 0): wgs0[:]}

        w1_codes = [keep.tile([P, PACK, P], U32, name=f"w1_codes{a}", align_bytes=64) for a in range(PASSES)]
        w1_plane = [keep.tile([P, PACK, P], U8, name=f"w1_plane{a}", align_bytes=64) for a in range(PASSES)]

        def quantise_w1(a, slices, dealt):
            there = slice(slices.start, slices.stop)
            nc.vector.quantize_mx(
                out=w1_codes[a][:, there, :].rearrange("p t m -> p (t m)").bitcast(E4M3X4),
                scales=w1_plane[a][:, there, :].rearrange("p t m -> p (t m)"),
                in_=dealt.rearrange("p t m u -> p (t m u)").bitcast(BF16),
            )

        def weave_and_deal(a, slices, copy, word):
            woven = ring.tile([P, H, PACK], BF16, name="w1_woven", tag="w1_woven", align_bytes=64)
            copy(woven[:].rearrange("p (c n) i -> p c i n", n=4), w1_raw[a][:].rearrange("p i (c n) -> p c i n", n=4))
            words = woven[:].rearrange("p c i -> p (c i)").bitcast(word).rearrange("p (m t u) -> p t m u", t=PACK, u=2)
            dealt = ring.tile([P, len(slices), P, 2], word, name="w1_dealt", tag="w1_dealt", align_bytes=64)
            copy(dealt[:], words[:, slices.start : slices.stop])
            return dealt

        quantise_w1(0, range(0, PACK), weave_and_deal(0, range(0, PACK), nc.vector.tensor_copy, I32)[:])
        gather_words(1)
        weights.update(load_wgs("wgs1", 48, range(1, 2), 0, S))
        pages.append(load_page(1, 0))
        pages.append(load_page(2, 16))
        weights.update(load_wgs("wgs2", 24, range(2, 3), 0, S))
        first = keep.tile([P, P, PACK], BF16, align_bytes=64)
        nc.vector.tensor_copy(first[:], w1_raw[1][:].rearrange("p i (m t) -> p m i t", t=PACK)[:, :, :, 0])
        quantise_w1(1, range(0, 1), first[:].rearrange("p m i -> p (m i)").bitcast(I32).rearrange("p (t m u) -> p t m u", t=1, u=2))
        woven = keep.tile([P, H, PACK], BF16, align_bytes=64)
        for c0, c1 in ((0, P), (P, H)):
            nc.vector.tensor_copy(
                woven[:, c0:c1].rearrange("p (c n) i -> p c i n", n=4),
                w1_raw[1][:, :, c0:c1].rearrange("p i (c n) -> p c i n", n=4),
            )
        words = woven[:].rearrange("p c i -> p (c i)").bitcast(I32).rearrange("p (m t u) -> p t m u", t=PACK, u=2)
        groups = (range(1, 2), range(2, PACK))
        dealt = [ring.tile([P, len(g), P, 2], I32, name="dealt", tag=f"dealt{g.start}", align_bytes=64) for g in groups]
        for g, tile in zip(groups, dealt):
            nc.vector.tensor_copy(tile[:], words[:, g.start : g.stop])
        for g, tile in zip(groups, dealt):
            quantise_w1(1, g, tile[:])

        pages.append(load_page(3, 33))
        weights.update(load_wgs("wgs3", 60, range(3, PACK), 0, S))
        w3 = place("w3", [P, N], U32, 28)
        nc.sync.dma_start(w3[:].bitcast(I32), w3_words[0].rearrange("p c i -> p (c i)").bitcast(I32))

        def first_product(bank, first, codes, planes):
            count = bank.shape[1]
            for a in range(PASSES):
                for c0 in range(0, count, P):
                    half, c1 = divmod(first + c0, HALF)
                    nc.tensor.matmul_mx(
                        out=bank[:, c0 : c0 + P],
                        lhsT=v_words[a, half][:, c1 : c1 + P].bitcast(E4M3X4),
                        lhsT_scale=v_plane[:, a, first + c0 : first + c0 + P],
                        rhs=codes[a],
                        rhs_scale=planes[a],
                        start=(a, c0) == (0, 0),
                        stop=(a, c0) == (PASSES - 1, count - P),
                    )

        def view(t, first, count, number, codes, planes, sign, tag, bufs):
            bank = new_bank(count, number)
            first_product(bank[:], first, codes(t), planes(t))
            if (t, first, tag) == (PACK - 1, HALF, "plus"):
                tanh = place("last_plus", [P, 7 * count], F32, ROUNDED)[:, :count]
            else:
                tanh = ring.tile([P, count], F32, name=tag, tag=tag, bufs=bufs)
            nc.scalar.activation(tanh[:], bank[:], ACT.Tanh, scale=sign)
            return tanh

        def w1_view(t, first, count, number):
            return view(
                t, first, count, number, lambda t: [w1_codes[a][:, t, :].bitcast(E4M3X4) for a in range(PASSES)],
                lambda t: [w1_plane[a][:, t, :] for a in range(PASSES)], 1.0, "plus", 4,
            )

        def w2_view(t, first, count, number):
            return view(
                t, first, count, number,
                lambda t: [w2_codes[:, a, t].rearrange("p m e -> p (m e)").bitcast(E2M1X4) for a in range(PASSES)],
                lambda t: [w2_dealt[:, a, t, :] for a in range(PASSES)], -1.0, "minus", BLOCKS,
            )

        def difference(h, t, first, minus, plus, number):
            count = plus.shape[1]
            bank = new_bank(count, number)
            for u, term in enumerate((minus, plus)):
                for c0 in range(0, count, P):
                    nc.tensor.matmul(
                        bank[:, c0 : c0 + P], lhsT=term[:, c0 : c0 + P], rhs=identity[:], is_transpose=True,
                        start=(u, c0) == (0, 0), stop=(u, c0) == (1, count - P),
                    )
            gain_t, wgs_t = gains[:, t : t + 1], weights[t, 0][:, first : first + count]
            if (t, first) == (0, 0):
                nc.vector.scalar_tensor_tensor(h, bank[:], gain_t, wgs_t, ALU.mult, ALU.mult)
            else:
                nc.scalar.activation(h, bank[:], ACT.Copy, scale=gain_t)
                nc.gpsimd.tensor_tensor(h, h, wgs_t, ALU.mult)

        def scatter(t, first, h):
            nc.vector.tensor_copy(pages[t][:].indirect(scatter_list[:, entries(first, h.shape[1])]), h)

        minus = w2_view(0, 0, HALF, 0)
        plus = [w1_view(0, u * FIRST, FIRST, 1 + u) for u in range(2)]
        for u in range(2):
            h = ring.tile([P, FIRST], F32, name="h0", tag=f"h0_{u}", align_bytes=64)
            difference(h[:], 0, u * FIRST, minus[:, u * FIRST : (u + 1) * FIRST], plus[u][:], 3 + u)
            scatter(0, u * FIRST, h[:])
        h = ring.tile([P, HALF], F32, name="h0", tag="h0_2", align_bytes=64)
        difference(h[:], 0, HALF, w2_view(0, HALF, HALF, 5)[:], w1_view(0, HALF, HALF, 6)[:], 1)
        scatter(0, HALF, h[:])
        w3_plane = ring.tile([P, 1, N], U8, name="w3_plane", tag="dealt2", align_bytes=64)
        nc.gpsimd.memset(w3_plane[:].bitcast(I32), 0)
        load_scale_rows(nc.sync, w3_plane, w3_scales)
        for t in range(1, PACK):
            h = keep.tile([P, S], F32, name=f"h{t}", align_bytes=64)
            minus = [w2_view(t, u * HALF, HALF, VIEW_BANKS[(4 * t - 4 + u) % 5]) for u in range(2)]
            plus = [w1_view(t, u * HALF, HALF, VIEW_BANKS[(4 * t - 2 + u) % 5]) for u in range(2)]
            for u in range(2):
                difference(h[:, u * HALF : (u + 1) * HALF], t, u * HALF, minus[u][:], plus[u][:], DIFFERENCE_BANKS[(2 * t - 2 + u) % 3])
            scatter(t, 0, h[:])

        span = STORE_CHUNKS * BANK
        last = PACK - 1
        flat = place("flat", [P, 2, T2], BF16, ROUNDED)
        early = [place(f"early{k}", [P, QUARTER, PACK], BF16, ROUNDED + 8 + 2 * k)[:] for k in range(3)]
        joined = place("joined", [P, QUARTER - SHARED + span, PACK], BF16, 60)
        early.append(joined[:, :QUARTER])
        late = joined[:, QUARTER - SHARED :]
        quarters = [slice(c0, c0 + QUARTER) for c0 in range(0, span, QUARTER)]

        def round_on_gpsimd(out, rows):
            nc.gpsimd.tensor_scalar(out, rows, 1.0, 0.0, ALU.mult, ALU.add)

        def twice(rows):
            return rows.unsqueeze(2).to_broadcast([P, rows.shape[1], 2])

        for t in range(PACK):
            nc.sync.dma_start(out_rows[t], pages[t][:])
        for t in range(2):
            nc.scalar.copy(flat[:, t], pages[t][:])
        for k, cols in enumerate(quarters):
            nc.scalar.copy(early[k][:, :, :2], flat[:, :, cols].rearrange("p t c -> p c t"))
        round_on_gpsimd(late[:, SHARED:, :2], flat[:, :, span + SHARED :].rearrange("p t c -> p c t"))
        round_on_gpsimd(late[:, SHARED:, 2], pages[2][:, span + SHARED :])
        for k, cols in enumerate(quarters):
            if k < 2:
                nc.scalar.copy(early[k][:, :, 2:], twice(pages[2][:, cols]))
            else:
                nc.scalar.copy(early[k][:, :, 2], pages[2][:, cols])
        for k, cols in enumerate(quarters):
            copy = nc.vector.tensor_copy if k < 2 else nc.scalar.copy
            copy(early[k][:, :, last], pages[last][:, cols])

        page_codes = {0: keep.tile([P, span], U32, name="early_codes", align_bytes=64)}
        page_plane = keep.tile([P, T2], U8, align_bytes=64)
        codes_out = out_2[0].rearrange("p m t -> p (m t)").bitcast(I32)

        def quantise(c0, values):
            count = values.shape[1] // PACK
            codes = page_codes[c0 // span * span][:, c0 % span : c0 % span + count]
            nc.vector.quantize_mx(out=codes.bitcast(E4M3X4), scales=page_plane[:, c0 : c0 + count], in_=values)

        def store_codes(c0):
            nc.sync.dma_start(codes_out[:, c0 : c0 + span], page_codes[c0][:].bitcast(I32))

        turns = []

        def results(c0, n0, width):
            y = ring.tile([P, span], F32, name="y", tag="y", bufs=8)
            for c1 in range(0, span, width):
                e = new_bank(width, len(turns) % BANKS)
                turns.append(c1)
                nc.tensor.matmul_mx(
                    out=e[:],
                    lhsT=w3[:, n0 : n0 + P].bitcast(E4M3X4),
                    lhsT_scale=w3_plane[:, 0, n0 : n0 + P],
                    rhs=page_codes[c0][:, c1 : c1 + width].bitcast(E4M3X4),
                    rhs_scale=page_plane[:, c0 + c1 : c0 + c1 + width],
                    start=True,
                    stop=True,
                )
                if (c0, STORE_CHUNKS * n0 // P + c1 // BANK) == (0, HOLD):
                    square = ring.tile([P, width], F32, name="square", tag="held", align_bytes=64)
                else:
                    square = ring.tile([P, width], F32, name="minus", tag="minus", bufs=BLOCKS)
                nc.scalar.activation(square[:], e[:], ACT.Square)
                nc.vector.scalar_tensor_tensor(y[:, c1 : c1 + width], square[:], 1.0, e[:], ALU.add, ALU.mult)
            nc.sync.dma_start(out_0[n0 : n0 + P, c0 : c0 + span], y[:])

        for k, cols in enumerate(quarters):
            quantise(cols.start, early[k].rearrange("p c t -> p (c t)"))
        store_codes(0)
        round_on_gpsimd(late[:, :, last], pages[last][:, span:])
        round_on_gpsimd(late[:, :SHARED, :2], flat[:, :, span : span + SHARED].rearrange("p t c -> p c t"))
        round_on_gpsimd(late[:, :SHARED, 2], pages[2][:, span : span + SHARED])
        results(0, 0, QUARTER)
        for n0 in range(P, (HOLD // 2 + 1) * P, P):
            results(0, n0, BANK)
        page_codes[span] = ring.tile([P, span], U32, name="late_codes", tag="held", align_bytes=64)
        quantise(span, late.rearrange("p c t -> p (c t)"))
        store_codes(span)
        scales_out = out_3[0].rearrange("(q r) c -> r q c", r=SCALE_ROWS)
        for r in range(SCALE_ROWS):
            nc.sync.dma_start(scales_out[r].bitcast(I32), page_plane[r:P:QUADRANT, :].bitcast(I32))
        for n0 in range((HOLD // 2 + 1) * P, N, P):
            results(0, n0, BANK)
        for n0 in range(0, N, P):
            results(span, n0, BANK)
